import numpy as np, ml_dtypes
CORES = [2,6,10,14,18,22,26,30]
N = 8
import mx_ref
BF = ml_dtypes.bfloat16
def gcols(t, e):
    v = np.concatenate([t.reshape(8, 16, -1, 4), np.zeros((8, 16, 1, 4), BF)], axis=2)
    return np.ascontiguousarray(np.stack([v[g][:, e[g]] for g in range(8)])).reshape(128, -1)
def tile(rs):
    return np.stack(rs, axis=2).reshape(128, -1).astype(BF)
def cut(t, i, w=512):
    return t[:, w * i:w * i + w]
def pick(q, e):
    c = np.concatenate([q[0].reshape(128, -1, 4), np.zeros((128, 1, 4), np.uint8)], axis=1); s = np.concatenate([q[1], np.ones((16, 1), np.uint8)], axis=1)
    return (np.ascontiguousarray(c[:, e].reshape(128, -1)), np.ascontiguousarray(s[:, e]))
def join(*qs):
    return (np.concatenate([q[0] for q in qs], axis=1), np.concatenate([q[1] for q in qs], axis=1))
def put(q, e, v):
    c, s = q[0].reshape(128, -1, 4).copy(), q[1].copy(); c[:, e] = v[0].reshape(128, -1, 4); s[:, e] = v[1]
    return (c.reshape(128, -1), s)
def pk(c, s):
    return (np.ascontiguousarray(c), mx_ref.live(s))
def emit(q):
    return q[0], q[1]
def packed(v, rng):
    q = [mx_ref.quantize(np.ascontiguousarray(v[r])) for r in range(N)]
    return np.stack([a for a, b in q]), np.stack([mx_ref.plane(b, rng) for a, b in q])
def values_of_codes():
    e, c = np.zeros((128, 128, 4), np.float32), np.zeros((128, 2, 4), np.uint8)
    e[np.arange(128), np.arange(128), 0] = 1
    c[:127, :, 0] = np.arange(256).reshape(2, 128).T[:127]
    return mx_ref.matmul(mx_ref.quantize(e.reshape(128, 512).astype(BF)), (c.reshape(128, 8), np.full((16, 2), 127, np.uint8))).T.reshape(-1).astype(np.float64)
CODE_VALUE, SCALE_VALUE = values_of_codes(), 2.0 ** (np.arange(256) - 127.0)
def decode(q):
    return (CODE_VALUE[q[0]].reshape(16, 8, -1, 4) * SCALE_VALUE[q[1]][:, None, :, None] + 0.0).reshape(128, -1).astype(np.float32)
def f(rng, *shape):
    return mx_ref.flush((rng.standard_normal(shape, dtype=np.float32) * np.exp2(rng.integers(-2, 3, shape[:-1] + (1,)))).astype(BF))
def wide(rng, *shape, cols=0):
    v = rng.standard_normal(shape, dtype=np.float32) * np.exp2(rng.integers(-12, 13, shape)).astype(np.float32)
    if cols: v *= np.repeat(np.exp2(rng.integers(-cols, cols + 1, shape[:-2] + (1, shape[-1] // 4))) * (rng.random(shape[:-2] + (1, shape[-1] // 4)) > 0.0625), 4, axis=-1).astype(np.float32)
    return mx_ref.flush(v.astype(BF))
C, A, K, R = 384, 128, 160, 3
STEP = [2, 5, 7]
def order(p):
    return np.argsort(-(p[::16] + np.float32(0.0)), axis=1, kind="stable")
def gput(t, e, h):
    a, b = t.reshape(8, 16, -1, 4).copy(), h.reshape(8, 16, -1, 4)
    for g in range(8): a[g][:, e[g]] = b[g]
    return a.reshape(128, -1)
def parts(m):
    return np.repeat(np.repeat(m, 16, axis=0), 4, axis=1)
def big(v):
    v = v.astype(np.float32)
    v[np.abs(v) < np.float32(2.0 ** -16)] = 0
    return v.astype(BF)
def numbers_of(rng):
    return {"x": big(f(rng, N, 128, 4 * C)), "u": np.array(f(rng, N, 128, 512)), "v": np.array(f(rng, N, 128, 512))}
def layers(rng):
    return big(f(rng, N, 128, 2048)).reshape(N, 8, 16, 4, 8, 16, 4)
def weights(rng, w):
    c, p = packed(np.ascontiguousarray(w).reshape(N, 128, 2048), rng)
    return {"wc": c, "ws": p}
def signs(rng):
    return np.stack([rng.permutation(8) % 2 * 2.0 - 1.0 for r in range(N)])
def setup_inputs(rng):
    return {**numbers_of(rng), **weights(rng, layers(rng))}
def setup_inputs_ties(rng):
    d = numbers_of(rng)
    e = rng.permutation(N)
    x = d["x"].reshape(N, 8, 16, C, 4)
    for r in range(N):
        k = np.zeros(C, int) if r == e[0] else rng.permutation(C) % 3
        a = x[r][:, :8, :3].copy()
        a[:, :, 2] = 0
        x[r][:, :8] = a[:, :, k]
    x[e[1]] = 0
    u = d["u"].reshape(N, 8, 16, 128, 4)
    u[:, :, 8:, ::16] = 0
    w = layers(rng)
    w[:, :, 8:, :, :, :8] = 0
    return {"x": x.reshape(N, 128, 4 * C), "u": u.reshape(N, 128, 512), "v": d["v"], **weights(rng, w)}
def setup_inputs_near(rng):
    d = numbers_of(rng)
    x = np.zeros((N, 8, 16, C, 4), np.float32)
    u = d["u"].reshape(N, 128, 128, 4)
    u[:, :, ::16] = 0
    o, c = rng.permutation(N) % 4, signs(rng)
    upper = np.arange(C) // (C // 2)
    for r in range(N):
        i = (np.arange(C) + rng.integers(0, C, (8, 1))) % C
        if o[r] == 3: i = i % (C // 2) * 2 + upper
        s = (i + 1) // 2
        size = 1.0 if o[r] < 2 else 2.0 ** -4
        g = ((s[:, :, None] >> np.arange(8)) & 1) * np.exp2(np.arange(8) - 23.0) * size
        if o[r] < 2: x[r, :, 0, :, 0] = c[r][:, None]
        if o[r] == 3: x[r, :, 0, :, 0] = (8 + upper) * 2.0 ** -30
        x[r, :, 8] = g[:, :, :4]
        x[r, :, 9] = g[:, :, 4:]
        x[r, :, 10:] = rng.integers(4, 8, (8, 6, C, 4)) * 2.0 ** -20 * size
        k = 1.0 if o[r] == 0 else 2.0 ** -30
        for h in range(0, 128, 16):
            u[r, h, h, 0] = k
            u[r, h + 8:h + 10, h] = k
    w = layers(rng)
    w[:, :, :10] = 0
    w[:, :, :, :, :, :10] = 0
    return {"x": x.reshape(N, 128, 4 * C).astype(BF), "u": u.reshape(N, 128, 512), "v": d["v"], **weights(rng, w)}
def setup_inputs_huge(rng):
    d = numbers_of(rng)
    c = np.stack([rng.permutation(C) % 2 * 2.0 - 1.0 for r in range(N)])
    c[rng.permutation(N) < N // 2] = -1
    x = (0.6 + 0.2 * rng.random((N, 128, C, 4))) * np.where(c < 0, -2.0 ** 30, 2.0 ** 28)[:, None, :, None]
    u = d["u"].reshape(N, 128, 128, 4)
    a = 2.0 ** 30 * (1 - 0.25 * rng.random((N, 128, 8, 4))) * signs(rng)[:, None, :, None]
    u[:, :, ::16] = a.astype(np.float32).astype(BF)
    w = np.zeros((N, 128, 4, 128, 4), np.float32)
    i = np.arange(128)
    for b in range(4): w[:, i, b, i, b] = 16
    return {"x": x.astype(np.float32).reshape(N, 128, 4 * C).astype(BF), "u": u.reshape(N, 128, 512), "v": d["v"], **weights(rng, w.astype(BF))}
def setup_inputs_slots(rng):
    d = numbers_of(rng)
    s = np.zeros((N, 8, C), bool)
    h = int(rng.integers(8))
    for r in range(N):
        p = r ^ STEP[0]
        if r < p:
            n = rng.permutation(np.array([K, K - 1, K + 1, 2 * A, A, rng.integers(A, 2 * A + 1), rng.integers(A, 2 * A + 1)]))
            n = np.insert(n, h, A)
            for g in range(8):
                e = rng.permutation(C)
                s[r, g, e[:A]] = True
                s[p, g, e[n[g] - A:n[g]]] = True
    s[:, h] = np.isin(np.arange(C), rng.permutation(C)[:A])
    k = (s * rng.integers(8, 16, (N, 8, C)) * 0.125).astype(np.float32).astype(BF)
    x = d["x"].reshape(N, 8, 16, C, 4)
    x[:, :, :8] = 0
    u = d["u"].reshape(N, 128, 128, 4)
    u[:, :, ::16] = 0
    for r in range(N):
        x[:, :, r, :, 0] = k[r]
        for g in range(8): u[r, 16 * g + r, 16 * g, 0] = 1
    w = layers(rng)
    w[:, :, :, :, :, :8] = 0
    return {"x": x.reshape(N, 128, 4 * C), "u": u.reshape(N, 128, 512), "v": d["v"], **weights(rng, w)}
def setup_inputs_spread(rng):
    d = setup_inputs(rng)
    d["x"] = big(wide(rng, N, 128, 4 * C, cols=6))
    return d
def check_inputs(d):
    b = []
    for k in ("x", "u", "v"):
        a = np.abs(d[k].astype(np.float32))
        if not (np.isfinite(a).all() and ((a == 0) | (a >= 2.0 ** -30) & (a <= 2.0 ** 30)).all()): b.append("a value of " + k)
    none, least, most = [emit(mx_ref.quantize(np.full((128, 16), k, np.float32).astype(BF)))[1][0, 0] for k in (0.0, 2.0 ** -30, 2.0 ** 30)]
    for r in range(N):
        if ((d["wc"][r] == 0x7F) | (d["wc"][r] == 0xFF)).any(): b.append("wc: a code that is no number")
        s = mx_ref.live(d["ws"][r])
        if ((s != none) & ((s < least) | (s > most))).any(): b.append("ws: a scale out of range")
    return b
def reference(x, u, v, wc, ws):
    qu = [mx_ref.quantize(u[r]) for r in range(N)]
    lay = [pk(wc[r], ws[r]) for r in range(N)]
    now = [x[r] for r in range(N)]
    vec = np.zeros((N, 8, C, N), np.int64)
    for t in range(R):
        sent = []
        for r in range(N):
            e = order(mx_ref.matmul(qu[r], mx_ref.quantize(now[r])))[:, :A]
            z = gcols(now[r], e)
            q = mx_ref.quantize(z)
            h = tile([np.maximum(mx_ref.matmul(pick(lay[r], np.arange(128 * b, 128 * b + 128)), q), np.float32(0.0)) * np.float32(0.03125) + z[:, b::4].astype(np.float32) for b in range(4)])
            now[r] = gput(now[r], e, h)
            for g in range(8): vec[r, g, e[g], r] += 1
            sent.append(mx_ref.quantize(now[r]))
        came = decode(join(*sent)).astype(BF)
        had = vec.copy()
        for r in range(N):
            p = r ^ STEP[t]
            want = (had[p] > had[r]).any(axis=2)
            for g in range(8): want[g, np.flatnonzero(want[g])[K:]] = False
            newer = (had[p] >= had[r]).all(axis=2)
            c = cut(came, p, 4 * C)
            half = ((now[r].astype(np.float32) + c.astype(np.float32)) * np.float32(0.5)).astype(BF)
            new = now[r].copy()
            a, b = parts(want & newer), parts(want & ~newer)
            new[a] = c[a]
            new[b] = half[b]
            now[r] = new
            vec[r][want] = np.maximum(had[r], had[p])[want]
    y, ov = np.zeros((N, 128, C), np.float32), np.zeros((N, 8, C), np.float32)
    oc, osc = np.zeros((N, 128, 4 * C), np.uint8), np.zeros((N, 16, C), np.uint8)
    for r in range(N):
        q = mx_ref.quantize(now[r])
        y[r] = mx_ref.matmul(mx_ref.quantize(v[r]), q)
        ov[r] = np.sum(vec[r] * 4 ** np.arange(N), axis=2)
        oc[r], osc[r] = emit(q)
    return {"y": y, "ov": ov, "oc": oc, "osc": osc}

@@ -1,0 +1,454 @@
+from concourse.mybir import dt, AluOpType, ActivationFunctionType
+
+STEP = [2, 5, 7]
+C, A, K, R = 384, 128, 160, 3
+NV = 14
+NS = 24 - NV
+GUARD = 0x4444
+Q4 = "float8_e4m3fn_x4"
+
+
+def _sb(n, d="float32"):
+    return ("sbuf", [128, n], d)
+
+
+BF, I32, U16, U8 = "bfloat16", "int32", "uint16", "uint8"
+SCRATCH = {
+    "win0": _sb(4 * 768, BF), "win1": _sb(4 * 1536, BF), "win2": _sb(4 * 1536, BF), "xlast": _sb(4 * C, BF),
+    "xh": _sb(4 * C, BF), "zt": _sb(512, BF), "oh": _sb(512, BF), "rr": _sb(512), "ut": _sb(512, BF), "vt": _sb(512, BF),
+    "qu": _sb(128, Q4), "su": _sb(128, U8), "qur": _sb(128, Q4), "sur": _sb(128, U8), "qv": _sb(128, Q4), "sv": _sb(128, U8),
+    "qw": _sb(512, Q4), "sw": _sb(512, U8), "qe": _sb(512, Q4), "se": _sb(512, U8), "qz": _sb(128, Q4), "sz": _sb(128, U8),
+    "et": _sb(2048, BF), "half": _sb(128, BF), "ident": _sb(128, BF),
+    "i8": _sb(8, I32), "uoff": _sb(8, U16), "i384": _sb(C, I32), "j384": _sb(C, I32), "i128": _sb(128, I32), "j128": _sb(128, I32),
+    "ip": _sb(1, I32), "jp": _sb(2, I32), "sel": _sb(C), "keep": _sb(C, BF),
+    "sel4": _sb(128), "keep4": _sb(128), "ids": _sb(C), "w4": _sb(192), "tab": _sb(16, BF),
+    "cat": _sb(2 * C), "ab": _sb(C), "pm": _sb(C), "tb": _sb(C), "eq": _sb(C, BF), "eqs": _sb(C, BF),
+    "mv": _sb(NV * C, BF), "sc": _sb(NV * 192, BF), "ms": _sb(NS * C, BF),
+    "ranku": _sb(24, U16), "inv": _sb(C), "p4": _sb(128), "s4": _sb(128),
+    "xoff": _sb(96, U16), "foff": _sb(96, U16), "dd": _sb(72, I32), "an": _sb(48, I32), "nwu": _sb(24, U16),
+    "wr": _sb(C, BF), "pre": _sb(C, BF), "sg": _sb(C, BF),
+    "un": _sb(192, I32), "uf": _sb(192), "ug": _sb(192), "ovb": _sb(32), "ovt": _sb(32), "ysb": _sb(C),
+}
+SMALL = {}
+for _n, _w in (("fp", 2), ("acc", 1), ("gm", 48), ("pp", 48), ("lc", NS)) + tuple((_k, 24) for _k in (
+        "f24", "c128", "c2", "base", "cc", "rank", "t1", "t2", "own", "wq", "pk", "fl", "mf", "a1", "a2", "b1", "cut",
+        "recv", "d1", "src", "inc")):
+    SMALL[_n] = (48 * len(SMALL), _w)
+SCRATCH["small"] = _sb(48 * len(SMALL))
+for _t in range(R + 1):
+    SCRATCH["qx%d" % _t], SCRATCH["sx%d" % _t] = _sb(C, Q4), _sb(C, U8)
+for _t in range(R):
+    SCRATCH["qh%d" % _t], SCRATCH["sh%d" % _t] = _sb(A, Q4), _sb(A, U8)
+    SCRATCH["lqh%d" % _t], SCRATCH["lsh%d" % _t] = _sb(A, Q4), _sb(A, U8)
+    SCRATCH["msg%d" % _t], SCRATCH["lmsg%d" % _t] = _sb(56, U16), _sb(56, U16)
+for _t in (1, 2):
+    SCRATCH["lqx%d" % _t], SCRATCH["lsx%d" % _t] = _sb(C, Q4), _sb(C, U8)
+    SCRATCH["cnt%d" % _t], SCRATCH["lcnt%d" % _t] = _sb(48, U16), _sb(48, U16)
+for _b in range(8):
+    SCRATCH["ps%d" % _b] = ("psum", [128, 512], "float32")
+
+SEMAPHORES = ["V", "S", "P", "G", "ldx", "ldu", "ldv", "ldw", "sent", "outy", "outs",
+              "ah0", "ah1", "ah2", "am0", "am1", "am2", "ax1", "ax2", "ac1", "ac2"]
+
+
+def rank_program(g, core, T, topo):
+    rank = T.rank_of(core)
+    if rank is None:
+        return
+    Op, Fn = AluOpType, ActivationFunctionType
+    queues = {"V": g.vector, "S": g.scalar, "P": g.tensor, "G": g, "Y": g.sync}
+    known = {q: {} for q in queues}
+    count = {}
+    seen = {}
+
+    def v(name, a=None, b=None, s=None):
+        if name in SMALL:
+            r = range(SMALL[name][0], sum(SMALL[name]))[a:b:s]
+            name = "small"
+        else:
+            r = range(T[name].shape[1])[a:b:s]
+        t = T[name]
+        if name.startswith("ps"):
+            m = 1
+        elif r.step == 1:
+            m = ((1 << len(r)) - 1) << r.start
+        else:
+            m = sum(1 << i for i in r)
+        ap = t[:, r.start:r.stop] if r.step == 1 else t[:, r.start:r.stop:r.step]
+        return (ap, [(name, m)])
+
+    def ind(win, off, words=False):
+        ap = win[0].bitcast(dt.uint32) if words else win[0]
+        return (ap.indirect(off[0]), win[1] + off[1])
+
+    def wait(q, sem, val, clock=None):
+        if known[q].get(sem, 0) < val:
+            queues[q].wait_ge(T.sem[sem], val)
+            known[q][sem] = val
+        for s, n in (clock or {}).items():
+            if known[q].get(s, 0) < n:
+                known[q][s] = n
+
+    def before(q, reads, writes):
+        need = []
+        for acc, wr in ((reads, False), (writes, True)):
+            for name, m in acc:
+                for e in seen.get(name, []):
+                    if e[0] & m and (wr or e[1] or (name.startswith("ps") and e[2] != q)):
+                        need.append(e)
+        for e in sorted(need, key=lambda e: -e[4]):
+            wait(q, e[3], e[4], e[5])
+
+    def after(q, reads, writes, sem, val):
+        clock = dict(known[q])
+        for name, m in writes:
+            seen[name] = [e for e in seen.get(name, []) if e[0] & ~m] + [[m, True, q, sem, val, clock]]
+        for name, m in reads:
+            seen.setdefault(name, []).append([m, False, q, sem, val, clock])
+
+    def run(q, call, out, ins, also=None):
+        reads = [x for i in ins if isinstance(i, tuple) for x in i[1]]
+        writes = list(out[1]) + (list(also[1]) if also else [])
+        before(q, reads, writes)
+        count[q] = count.get(q, 0) + 1
+        call().then_inc(T.sem[q], 1)
+        after(q, reads, writes, q, count[q])
+
+    def ap(x):
+        return x[0] if isinstance(x, tuple) else x
+
+    def cp(out, in_):
+        run("V", lambda: g.vector.tensor_copy(out[0], in_[0]), out, [in_])
+
+    def scatter(win, off, in_):
+        run("V", lambda: g.vector.tensor_copy(win[0].indirect(off[0]), in_[0]), win, [off, in_])
+
+    def tt(out, a, b, op):
+        run("V", lambda: g.vector.tensor_tensor(out[0], a[0], b[0], op), out, [a, b])
+
+    def ts(out, a, s1, op0, s2=None, op1=None):
+        if op1 is None:
+            run("V", lambda: g.vector.tensor_scalar(out[0], a[0], ap(s1), None, op0), out, [a, s1])
+        else:
+            run("V", lambda: g.vector.tensor_scalar(out[0], a[0], ap(s1), ap(s2), op0, op1), out, [a, s1, s2])
+
+    def scan(out, d0, d1, init, op0, op1):
+        run("V", lambda: g.vector.tensor_tensor_scan(out[0], d0[0], d1[0], init, op0, op1), out, [d0, d1])
+
+    def fill(out, c):
+        run("V", lambda: g.vector.memset(out[0], c), out, [])
+
+    def quant(q, s, in_):
+        run("V", lambda: g.vector.quantize_mx(q[0], s[0], in_[0]), q, [in_], s)
+
+    def act(out, in_, fn, bias=None, scale=1.0, acc=None):
+        kw = {"scale": scale}
+        if bias is not None:
+            kw["bias"] = ap(bias)
+        if acc is not None:
+            kw["accum_out"] = acc[0]
+        run("S", lambda: g.scalar.activation(out[0], in_[0], fn, **kw), out, [in_, bias], acc)
+
+    def mm(bank, n, lq, ls, rq, rs):
+        out = v("ps%d" % bank, 0, n)
+        run("P", lambda: g.tensor.matmul_mx(out[0], lq[0], ls[0], rq[0], rs[0], True, True), out, [lq, ls, rq, rs])
+
+    def iota(out, pattern, base, mult, real=False):
+        if real:
+            run("G", lambda: g.iota(out[0], pattern, base, mult, allow_small_or_imprecise_dtypes=True), out, [])
+        else:
+            run("G", lambda: g.iota(out[0], pattern, base, mult), out, [])
+
+    def dma(q, out, in_, sem, reads=(), writes=(), last=None):
+        before(q, list(reads), list(writes))
+        count[sem] = count.get(sem, 0) + 16
+        queues[q].dma_start(out, in_).then_inc(T.sem[sem], 16)
+        after(q, list(reads), list(writes), sem, last or count[sem])
+
+    def send(peer, dst, src, sem, codes=False):
+        before("G", src[1], [])
+        rid, pid, _ = topo.addr(peer)
+        o, i = (dst[0].bitcast(dt.uint8), src[0].bitcast(dt.uint8)) if codes else (dst[0], src[0])
+        g.remote_dma(o, i, T.sem[sem], T.sem["sent"], pid, rid, topo.mask(core, peer))
+        count["sent"] = count.get("sent", 0) + len(topo.engines(core, peer))
+
+    def lands(peer, names, sem):
+        n = len(names) * len(topo.engines(peer, core))
+        for name in names:
+            seen[name] = [[v(name)[1][0][1], True, None, sem, n, {}]]
+
+    peers = [T.cores[rank ^ s] for s in STEP]
+    coset = [0] + STEP
+    first = min(rank ^ d for d in coset)
+    high = sorted((rank ^ d for d in coset), reverse=True)
+    for t in range(R):
+        lands(peers[t], ["lqh%d" % t, "lsh%d" % t], "ah%d" % t)
+        lands(peers[t], ["lmsg%d" % t], "am%d" % t)
+        if t:
+            lands(peers[t], ["lcnt%d" % t], "ac%d" % t)
+            lands(peers[t], ["lqx%d" % t, "lsx%d" % t], "ax%d" % t)
+
+    def field(r):
+        return float(16 ** coset.index(r ^ first))
+
+    x0 = v("win0", 512, 2048)
+    dma("S", x0[0], T.x[:], "ldx", writes=x0[1])
+    dma("Y", v("ut")[0], T.u[:], "ldu", writes=v("ut")[1])
+    before("Y", x0[1], [])
+    dma("Y", v("qw")[0].bitcast(dt.uint8), T.wc[:], "ldw", writes=v("qw")[1], last=32)
+    dma("Y", v("sw")[0], T.ws[:], "ldw", writes=v("sw")[1], last=32)
+    dma("Y", v("vt")[0], T.v[:], "ldv", writes=v("vt")[1])
+    iota(v("i8"), [[16, 8]], 0, 0)
+    iota(v("i384"), [[0, 24], [1, 16]], 128, -1)
+    iota(v("ip"), [[0, 1]], 0, 1)
+    iota(v("i128"), [[0, 32], [-4, 4]], 128, 1)
+    iota(v("f24"), [[16, 24]], 128, 0, True)
+    iota(v("ids"), [[4, C]], 0, 0, True)
+    fill(v("half"), 0.5)
+    run("G", lambda: g.affine_select(v("ident")[0], v("half")[0], [[-1, 128]], Op.is_equal, 0.0, 0, 1), v("ident"), [v("half")])
+    fill(v("et"), 0.0)
+    cp(v("uoff"), v("i8"))
+    ts(v("j384"), v("i384"), 15, Op.bitwise_and)
+    fill(v("base", 0, NV), 192.0)
+    fill(v("base", NV, 24), 384.0)
+    ts(v("sel"), v("j384"), 0.0, Op.is_equal)
+    ts(v("keep"), v("j384"), 0.0, Op.not_equal)
+    quant(v("qu"), v("su"), v("ut"))
+    cp((v("qur")[0].bitcast(dt.uint32), v("qur")[1]), ind(v("qu"), v("uoff"), True))
+    cp(v("sur"), ind(v("su"), v("uoff")))
+    ts(v("j128"), v("i128"), 15, Op.bitwise_and)
+    ts(v("jp", 0, 1), v("ip"), 15, Op.bitwise_and)
+    ts(v("jp", 1, 2), v("ip"), 3, Op.bitwise_and)
+    ts(v("sel4"), v("j128"), 4.0, Op.is_lt)
+    quant(v("qx0"), v("sx0"), x0)
+    cp(v("fp"), v("jp"))
+    ts(v("keep4"), v("j128"), 4.0, Op.is_ge)
+    ts(v("c128"), v("f24"), v("fp", 0, 1), Op.add)
+    fill(v("pk"), 0.0)
+
+    def half_tile(b):
+        return v("qe", 128 * b, 128 * b + 128), v("se", 128 * b, 128 * b + 128)
+
+    def offsets(name, src, b):
+        ts(v(name, 24 * b, 24 * b + 24), v(src), 4.0, Op.mult, float(b), Op.add)
+
+    def sign(k):
+        j = k - NV
+        act(v("ms", j * C, j * C + C), v("cat", 16 * k + 16, 16 * k + 400), Fn.Sign, v("tb", 16 * k + 15, 16 * k + 16), -1.0)
+
+    def lost(k):
+        j = k - NV
+        act(v("ms", j * C, j * C + C), v("ms", j * C, j * C + C), Fn.Relu, acc=v("lc", j, j + 1))
+
+    def compare(k):
+        ts(v("mv", k * C, k * C + C), v("cat", 16 * k + 16, 16 * k + 400), v("tb", 16 * k + 15, 16 * k + 16), Op.is_ge)
+
+    def total(k):
+        scan(v("sc", k * 192, k * 192 + 192), v("mv", k * C, k * C + 192), v("mv", k * C + 192, k * C + C), -192.0, Op.add, Op.add)
+
+    for t in range(R):
+        win = "win%d" % t
+        msg, lmsg, lcnt = "msg%d" % t, "lmsg%d" % t, "lcnt%d" % t
+        qx, sx = v("qx%d" % t), v("sx%d" % t)
+        mean = 128 if t == 0 else 512
+        wide = 768 if t == 0 else 1536
+
+        mm(4, C, v("qur"), v("sur"), qx, sx)
+        mm(5, C, v("qur"), v("sur"), qx, sx)
+        if t:
+            send(peers[t], v("lqx%d" % t), qx, "ax%d" % t, True)
+            send(peers[t], v("lsx%d" % t), sx, "ax%d" % t)
+        act(v("ab"), v("ps5", 0, C), Fn.Abs, 2.0 ** -124, 1.25 * 2.0 ** -24)
+        act(v("cat", C, 2 * C), v("ps5", 0, C), Fn.Copy)
+        tt(v("pm"), v("ps4", 0, C), v("sel"), Op.mult)
+        scan(v("tb"), v("keep"), v("pm"), 0.0, Op.mult, Op.add)
+        tt(v("cat", 0, C), v("ps4", 0, C), v("ab"), Op.subtract)
+        tt(v("eq"), v("ps4", 0, C), v("tb"), Op.is_equal)
+        if t:
+            for b in range(4):
+                mm(b, C, *half_tile(b), v("lqx%d" % t), v("lsx%d" % t))
+        ks = list(range(23, NV - 1, -1))
+        sign(ks[0])
+        for a, b in zip(ks, ks[1:]):
+            sign(b)
+            lost(a)
+        lost(ks[-1])
+        compare(0)
+        scan(v("eqs"), v("keep"), v("eq"), 0.0, Op.mult, Op.add)
+        for k in range(1, NV):
+            compare(k)
+            total(k - 1)
+            if k == 1:
+                tt(v("cc"), v("base"), v("eqs", 15, C, 16), Op.subtract)
+        total(NV - 1)
+        if t:
+            for b in range(4):
+                act(v(win, 4 * 640 + b, 4 * 1024, 4), v("ps%d" % b, 0, C), Fn.Copy, scale=2.0)
+        tt(v("rank", NV, 24), v("cc", NV, 24), v("lc"), Op.subtract)
+        tt(v("rank", 0, NV), v("sc", 191, NV * 192, 192), v("cc", 0, NV), Op.add)
+        place = v("cnt%d" % t, 0, 24) if t else v("ranku")
+        cp(place, v("rank"))
+        if t:
+            send(peers[t], v(lcnt), v("cnt%d" % t), "ac%d" % t)
+        scatter(v("inv"), place, v("ids"))
+        tt(v("p4"), v("inv", 0, 128), v("sel4"), Op.mult)
+        scan(v("s4"), v("keep4"), v("p4"), 0.0, Op.mult, Op.add)
+        ts(v(msg, 0, 32), v("s4", 3, 128, 4), v("fp", 1, 2), Op.add)
+
+        xs = v(win, 512, 2048)
+        act(v("zt", 256, 512), ind(xs, v(msg, 16, 32)), Fn.Copy)
+        cp(v("zt", 0, 256), ind(xs, v(msg, 0, 16)))
+        ts(v("t1"), v("rank"), -127.0, Op.add, 1000.0, Op.mult)
+        quant(v("qz"), v("sz"), v("zt"))
+        for b in range(4):
+            mm(4 + b, A, v("qw", 128 * b, 128 * b + 128), v("sw", 128 * b, 128 * b + 128), v("qz"), v("sz"))
+        for b in range(4):
+            act(v("rr", 128 * b, 128 * b + 128), v("ps%d" % (4 + b), 0, A), Fn.Relu, scale=0.03125)
+        tt(v("t2"), v("t1"), v("rank"), Op.max)
+        ts(v("wq"), v("rank"), 128.0, Op.is_lt, field(rank), Op.mult)
+        tt(v("own"), v("t2"), v("c128"), Op.min)
+        tt(v("pk"), v("pk"), v("wq"), Op.add)
+        cp(v(msg, 32, 56), v("own"))
+        send(peers[t], v(lmsg), v(msg), "am%d" % t)
+        offsets("xoff", "own", 1)
+        for b in range(4):
+            tt(v(win, b, 512, 4), v("rr", 128 * b, 128 * b + 128), v("zt", b, 512, 4), Op.add)
+        quant(v("qh%d" % t), v("sh%d" % t), v(win, 0, 512))
+        send(peers[t], v("lqh%d" % t), v("qh%d" % t), "ah%d" % t, True)
+        send(peers[t], v("lsh%d" % t), v("sh%d" % t), "ah%d" % t)
+
+        def halve(b, q):
+            src = ind(v(win, 0, 2048), v("xoff", 24 * b, 24 * b + 24))
+            if q == "V":
+                ts(v("xh", b, 4 * C, 4), src, 0.5, Op.mult)
+            else:
+                act(v("xh", b, 4 * C, 4), src, Fn.Copy, scale=0.5)
+
+        def mean_x(b):
+            tt(v(win, 4 * 1152 + b, 4 * 1536, 4), v("ps%d" % b, 0, C), v("xh", b, 4 * C, 4), Op.add)
+
+        halve(1, "S")
+        if t == 0:
+            for b in (0, 3, 2):
+                offsets("xoff", "own", b)
+            halve(0, "V")
+            halve(3, "S")
+            halve(2, "V")
+            act(v("oh"), ind(v("xh"), v(lmsg, 0, 32)), Fn.Copy)
+            for b in range(4):
+                cp(v("et", 513 * b, 512 * b + 512, 4), v("ident"))
+            ts(v("a1"), v("own"), 128.0, Op.is_lt, float(mean), Op.mult)
+            ts(v("mf"), v(lmsg, 32, 56), 512.0, Op.add)
+            quant(v("qe"), v("se"), v("et"))
+            tt(v("a2"), v("a1"), v("own"), Op.subtract)
+            ts(v("recv"), v("mf"), 640.0, Op.is_lt)
+        else:
+            ts(v("gm", 0, 24), v(lcnt, 0, 24), 128.0, Op.is_lt, field(rank ^ STEP[t]), Op.mult)
+            cp(v("gm", 24, 48), v(lcnt, 24, 48))
+            offsets("xoff", "own", 2)
+            tt(v("pp", 0, 24), v("gm", 0, 24), v("gm", 24, 48), Op.add)
+            offsets("xoff", "own", 0)
+            if t == 1:
+                ts(v("nwu"), v("pp", 0, 24), 0.0, Op.is_equal)
+                ts(v("fl"), v("pp", 0, 24), 0.0, Op.is_equal)
+                ts(v("a1"), v("pk"), 0.0, Op.is_gt, float(mean), Op.mult)
+                offsets("xoff", "own", 3)
+            else:
+                tt(v("pp", 24, 48), v("pp", 0, 24), v("pk"), Op.subtract)
+                offsets("xoff", "own", 3)
+                ts(v("dd", 48, 72), v("pp", 24, 48), -1.0, Op.mult, float(GUARD), Op.add)
+                ts(v("dd", 24, 48), v("pp", 24, 48), float(GUARD), Op.add)
+                ts(v("an", 24, 48), v("dd", 48, 72), GUARD, Op.bitwise_and)
+                ts(v("an", 0, 24), v("dd", 24, 48), GUARD, Op.bitwise_and)
+                ts(v("nwu"), v("an", 24, 48), float(GUARD), Op.is_equal)
+                ts(v("fl"), v("an", 24, 48), float(GUARD), Op.is_equal)
+                ts(v("a1"), v("an", 0, 24), float(GUARD), Op.not_equal, float(mean), Op.mult)
+                halve(2, "S")
+            act(v("wr"), ind(v("tab"), v("nwu")), Fn.Copy)
+            if t == 1:
+                halve(0, "V")
+                halve(2, "S")
+            else:
+                halve(0, "S")
+                mean_x(1)
+                mean_x(2)
+            tt(v("a2"), v("a1"), v("own"), Op.subtract)
+            scan(v("pre"), v("wr"), v("wr"), 0.0, Op.add, Op.max)
+            act(v("sg", K, C), v("pre", K, C), Fn.Sign, K + 0.5, -1.0, v("acc"))
+            halve(3, "S")
+            act(v("oh"), ind(v("xh"), v(lmsg, 0, 32)), Fn.Copy)
+            if t == 1:
+                mean_x(1)
+            mean_x(0)
+            ts(v("cut"), v("c2"), v("acc"), Op.is_lt)
+            if t == 1:
+                mean_x(2)
+            ts(v("mf"), v(lmsg, 32, 56), 512.0, Op.add)
+            tt(v("recv"), v("cut"), v("fl"), Op.is_gt)
+        tt(v("b1"), v("mf"), v("a2"), Op.add)
+        if t:
+            mean_x(3)
+        else:
+            quant(v("qv"), v("sv"), v("vt"))
+        tt(v("d1"), v("b1"), v("recv"), Op.mult)
+        tt(v("src"), v("d1"), v("own"), Op.add)
+        for b in range(4):
+            offsets("foff", "src", b)
+        if t == 0:
+            ts(v("c2"), v("c128"), 2.0, Op.mult, -256.0 - (C + K), Op.add)
+            fill(v("tab", 0, 1), 1.0)
+            fill(v("tab", 1, 16), 0.0)
+
+        for b in range(4):
+            mm(4 + b, A, *half_tile(b), v("lqh%d" % t), v("lsh%d" % t))
+            mm(b, A, *half_tile(b), v("lqh%d" % t), v("lsh%d" % t))
+        for b in range(4):
+            act(v(win, 4 * 512 + b, 4 * 640, 4), v("ps%d" % b, 0, A), Fn.Copy, scale=2.0)
+            o = 4 * (512 + mean)
+            tt(v(win, o + b, o + 512, 4), v("ps%d" % (4 + b), 0, A), v("oh", b, 512, 4), Op.add)
+        nxt, o = ("win%d" % (t + 1), 512) if t < R - 1 else ("xlast", 0)
+        for b in range(4):
+            out, src = v(nxt, o + b, o + 4 * C, 4), ind(v(win, 0, 4 * wide), v("foff", 24 * b, 24 * b + 24))
+            if b % 2:
+                act(out, src, Fn.Copy)
+            else:
+                cp(out, src)
+        quant(v("qx%d" % (t + 1)), v("sx%d" % (t + 1)), v(nxt, o, o + 4 * C))
+        if t < 2:
+            if t == 0:
+                ts(v("inc"), v("recv"), field(rank ^ STEP[0]), Op.mult)
+                fill(v("ovb", 24, 32), 0.0)
+                fill(v("w4", 1, 192, 2), 1.0)
+            else:
+                tt(v("inc"), v("cut"), v("pp", 0, 24), Op.mult)
+            for j in (2 * t, 2 * t + 1):
+                fill(v("w4", 2 * j, 192, 8), float(4 ** (high[j - 1] - high[j])) if j else 0.0)
+            tt(v("pk"), v("pk"), v("inc"), Op.add)
+            cp(v("cnt%d" % (t + 1), 24, 48), v("pk"))
+
+    qx, sx = v("qx%d" % R), v("sx%d" % R)
+    mm(4, C, v("qv"), v("sv"), qx, sx)
+    dma("Y", T.oc[:], qx[0].bitcast(dt.uint8), "outy", reads=qx[1])
+    for k in range(4):
+        dma("Y", T.osc[4 * k:4 * k + 4, :], T["sx%d" % R][32 * k:32 * k + 4, :], "outy", reads=sx[1])
+    act(v("ysb"), v("ps4", 0, C), Fn.Copy)
+    dma("S", T.y[:], v("ysb")[0], "outs", reads=v("ysb")[1])
+    tt(v("inc"), v("pp", 24, 48), v("recv"), Op.mult)
+    ts(v("dd", 0, 48, 2), v("pk"), float(GUARD), Op.add)
+    ts(v("dd", 1, 48, 2), v("inc"), float(GUARD), Op.add)
+    for j in range(4):
+        for h in range(2):
+            ts(v("un", 2 * j + h, 192, 8), v("dd", h, 48, 2), 4 * coset.index(high[j] ^ first), Op.logical_shift_right, 7, Op.bitwise_and)
+    ts(v("uf"), v("un"), -4.0, Op.add, 0.0, Op.max)
+    scan(v("ug"), v("w4"), v("uf"), 0.0, Op.mult, Op.add)
+    ts(v("ovb", 0, 24), v("ug", 7, 192, 8), float(4 ** high[3]), Op.mult)
+    run("V", lambda: g.vector.transpose(v("ovt")[0], v("ovb")[0]), v("ovt"), [v("ovb")])
+    for k in range(8):
+        q, sem = ("Y", "outy") if k % 2 else ("S", "outs")
+        a, h = k // 2, k % 2
+        dma(q, T.ov[k:k + 1, :], T["ovt"][32 * a:32 * a + 24, 16 * h:16 * h + 16], sem, reads=v("ovt")[1])
+    wait("G", "G", count["G"])
+    wait("G", "sent", count["sent"])
+    wait("P", "P", count["P"])
+    wait("Y", "outy", count["outy"])
+    wait("S", "outs", count["outs"])

@@ -2,9 +2,15 @@ from concourse.mybir import dt, AluOpType, ActivationFunctionType
 
 STEP = [2, 5, 7]
 C, A, K, R = 384, 128, 160, 3
-NV = 14
-NS = 24 - NV
+HC = C // 2
 GUARD = 0x4444
+FAR = 1e28
+B = 4096.0
+BB = 65536.0
+NF = 5120
+PIECES = [(828, 1280), (552, 828), (276, 552), (96, 276), (0, 128)]
+NHV = 0
+ZS = 256
 Q4 = "float8_e4m3fn_x4"
 
 
@@ -19,19 +25,20 @@ SCRATCH = {
     "qu": _sb(128, Q4), "su": _sb(128, U8), "qur": _sb(128, Q4), "sur": _sb(128, U8), "qv": _sb(128, Q4), "sv": _sb(128, U8),
     "qw": _sb(512, Q4), "sw": _sb(512, U8), "qe": _sb(512, Q4), "se": _sb(512, U8), "qz": _sb(128, Q4), "sz": _sb(128, U8),
     "et": _sb(2048, BF), "half": _sb(128, BF), "ident": _sb(128, BF),
-    "i8": _sb(8, I32), "uoff": _sb(8, U16), "i384": _sb(C, I32), "j384": _sb(C, I32), "i128": _sb(128, I32), "j128": _sb(128, I32),
-    "ip": _sb(1, I32), "jp": _sb(2, I32), "sel": _sb(C), "keep": _sb(C, BF),
-    "sel4": _sb(128), "keep4": _sb(128), "ids": _sb(C), "w4": _sb(192), "tab": _sb(16, BF),
-    "cat": _sb(2 * C), "ab": _sb(C), "pm": _sb(C), "tb": _sb(C), "eq": _sb(C, BF), "eqs": _sb(C, BF),
-    "mv": _sb(NV * C, BF), "sc": _sb(NV * 192, BF), "ms": _sb(NS * C, BF),
-    "ranku": _sb(24, U16), "inv": _sb(C), "p4": _sb(128), "s4": _sb(128),
-    "xoff": _sb(96, U16), "foff": _sb(96, U16), "dd": _sb(72, I32), "an": _sb(48, I32), "nwu": _sb(24, U16),
+    "ones": _sb(128, BF), "gb1": _sb(128, BF), "gb": _sb(128, BF), "bt": _sb(1024, BF), "qb": _sb(256, Q4), "sb": _sb(256, U8),
+    "i8": _sb(8, I32), "uoff": _sb(8, U16), "i192": _sb(HC, I32), "j192": _sb(HC, I32), "f128": _sb(128), "d128": _sb(128),
+    "ip": _sb(1, I32), "jp": _sb(2, I32), "far": _sb(HC), "reset": _sb(HC), "keep": _sb(C, BF),
+    "ma": _sb(128), "mb": _sb(128), "m4": _sb(128), "m96": _sb(96), "ids": _sb(C), "w4": _sb(192), "tab": _sb(16, BF),
+    "cat": _sb(560), "ab": _sb(HC), "pm": _sb(C), "tb": _sb(C), "ds": _sb(C, BF),
+    "mv": _sb(NF, BF), "qm": _sb(NF // 4 + 32, Q4), "sm": _sb(NF // 4 + 32, U8), "sc": _sb(24 * 96, BF), "ms": _sb(12 * 176, BF),
+    "rs": _sb(96), "inv": _sb(C), "s4": _sb(128),
+    "xoff": _sb(96, U16), "foff": _sb(96, U16), "dd": _sb(72, I32), "de": _sb(48, I32), "an": _sb(48, I32), "nwu": _sb(24, U16),
     "wr": _sb(C, BF), "pre": _sb(C, BF), "sg": _sb(C, BF),
     "un": _sb(192, I32), "uf": _sb(192), "ug": _sb(192), "ovb": _sb(32), "ovt": _sb(32), "ysb": _sb(C),
 }
 SMALL = {}
-for _n, _w in (("fp", 2), ("acc", 1), ("gm", 48), ("pp", 48), ("lc", NS)) + tuple((_k, 24) for _k in (
-        "f24", "c128", "c2", "base", "cc", "rank", "t1", "t2", "own", "wq", "pk", "fl", "mf", "a1", "a2", "b1", "cut",
+for _n, _w in (("fp", 2), ("acc", 1), ("gm", 48), ("pp", 48), ("lc", 12)) + tuple((_k, 24) for _k in (
+        "f24", "c128", "c2", "cm", "cc", "t1", "t2", "sw1", "own", "wq", "pk", "want", "mf", "a1", "b1", "b2", "cut",
         "recv", "d1", "src", "inc")):
     SMALL[_n] = (48 * len(SMALL), _w)
 SCRATCH["small"] = _sb(48 * len(SMALL))
@@ -40,15 +47,15 @@ for _t in range(R + 1):
 for _t in range(R):
     SCRATCH["qh%d" % _t], SCRATCH["sh%d" % _t] = _sb(A, Q4), _sb(A, U8)
     SCRATCH["lqh%d" % _t], SCRATCH["lsh%d" % _t] = _sb(A, Q4), _sb(A, U8)
-    SCRATCH["msg%d" % _t], SCRATCH["lmsg%d" % _t] = _sb(56, U16), _sb(56, U16)
+    SCRATCH["msg%d" % _t] = SCRATCH["lmsg%d" % _t] = _sb(56 if _t else 32, U16)
+    SCRATCH["cnt%d" % _t] = SCRATCH["lcnt%d" % _t] = _sb(48 if _t else 24, U16)
 for _t in (1, 2):
     SCRATCH["lqx%d" % _t], SCRATCH["lsx%d" % _t] = _sb(C, Q4), _sb(C, U8)
-    SCRATCH["cnt%d" % _t], SCRATCH["lcnt%d" % _t] = _sb(48, U16), _sb(48, U16)
 for _b in range(8):
     SCRATCH["ps%d" % _b] = ("psum", [128, 512], "float32")
 
 SEMAPHORES = ["V", "S", "P", "G", "ldx", "ldu", "ldv", "ldw", "sent", "outy", "outs",
-              "ah0", "ah1", "ah2", "am0", "am1", "am2", "ax1", "ax2", "ac1", "ac2"]
+              "ah0", "ah1", "ah2", "am0", "am1", "am2", "ax1", "ax2", "ac0", "ac1", "ac2"]
 
 
 def rank_program(g, core, T, topo):
@@ -89,12 +96,12 @@ def rank_program(g, core, T, topo):
             if known[q].get(s, 0) < n:
                 known[q][s] = n
 
-    def before(q, reads, writes):
+    def before(q, reads, writes, adds=False):
         need = []
         for acc, wr in ((reads, False), (writes, True)):
             for name, m in acc:
                 for e in seen.get(name, []):
-                    if e[0] & m and (wr or e[1] or (name.startswith("ps") and e[2] != q)):
+                    if e[0] & m and (wr or e[1] or (name.startswith("ps") and e[2] != q)) and not (adds and wr and e[2] == q):
                         need.append(e)
         for e in sorted(need, key=lambda e: -e[4]):
             wait(q, e[3], e[4], e[5])
@@ -106,10 +113,10 @@ def rank_program(g, core, T, topo):
         for name, m in reads:
             seen.setdefault(name, []).append([m, False, q, sem, val, clock])
 
-    def run(q, call, out, ins, also=None):
+    def run(q, call, out, ins, also=None, adds=False):
         reads = [x for i in ins if isinstance(i, tuple) for x in i[1]]
         writes = list(out[1]) + (list(also[1]) if also else [])
-        before(q, reads, writes)
+        before(q, reads, writes, adds)
         count[q] = count.get(q, 0) + 1
         call().then_inc(T.sem[q], 1)
         after(q, reads, writes, q, count[q])
@@ -149,15 +156,21 @@ def rank_program(g, core, T, topo):
             kw["accum_out"] = acc[0]
         run("S", lambda: g.scalar.activation(out[0], in_[0], fn, **kw), out, [in_, bias], acc)
 
-    def mm(bank, n, lq, ls, rq, rs):
+    def pick_scales(out, in_):
+        run("S", lambda: g.scalar.activation(out[0], in_[0], Fn.Copy), out, [in_])
+
+    def mm(bank, n, lq, ls, rq, rs, start=True, stop=True):
         out = v("ps%d" % bank, 0, n)
-        run("P", lambda: g.tensor.matmul_mx(out[0], lq[0], ls[0], rq[0], rs[0], True, True), out, [lq, ls, rq, rs])
+        run("P", lambda: g.tensor.matmul_mx(out[0], lq[0], ls[0], rq[0], rs[0], start, stop), out, [lq, ls, rq, rs], adds=not start)
 
     def iota(out, pattern, base, mult, real=False):
         if real:
             run("G", lambda: g.iota(out[0], pattern, base, mult, allow_small_or_imprecise_dtypes=True), out, [])
         else:
             run("G", lambda: g.iota(out[0], pattern, base, mult), out, [])
+
+    def select(out, in_, pattern, op, base, mult):
+        run("G", lambda: g.affine_select(out[0], in_[0], pattern, op, 0.0, base, mult), out, [in_])
 
     def dma(q, out, in_, sem, reads=(), writes=(), last=None):
         before(q, list(reads), list(writes))
@@ -184,67 +197,102 @@ def rank_program(g, core, T, topo):
     for t in range(R):
         lands(peers[t], ["lqh%d" % t, "lsh%d" % t], "ah%d" % t)
         lands(peers[t], ["lmsg%d" % t], "am%d" % t)
+        lands(peers[t], ["lcnt%d" % t], "ac%d" % t)
         if t:
-            lands(peers[t], ["lcnt%d" % t], "ac%d" % t)
             lands(peers[t], ["lqx%d" % t, "lsx%d" % t], "ax%d" % t)
 
     def field(r):
         return float(16 ** coset.index(r ^ first))
 
     x0 = v("win0", 512, 2048)
-    dma("S", x0[0], T.x[:], "ldx", writes=x0[1])
     dma("Y", v("ut")[0], T.u[:], "ldu", writes=v("ut")[1])
+    dma("S", x0[0], T.x[:], "ldx", writes=x0[1])
     before("Y", x0[1], [])
     dma("Y", v("qw")[0].bitcast(dt.uint8), T.wc[:], "ldw", writes=v("qw")[1], last=32)
     dma("Y", v("sw")[0], T.ws[:], "ldw", writes=v("sw")[1], last=32)
     dma("Y", v("vt")[0], T.v[:], "ldv", writes=v("vt")[1])
+    fill(v("ones"), 1.0)
     iota(v("i8"), [[16, 8]], 0, 0)
-    iota(v("i384"), [[0, 24], [1, 16]], 128, -1)
+    select(v("gb1"), v("ones"), [[-16, 8], [0, 16]], Op.is_ge, 0, 1)
+    select(v("gb"), v("gb1"), [[16, 8], [0, 16]], Op.is_ge, 15, -1)
+    iota(v("i192"), [[0, 12], [1, 16]], 128, -1)
     iota(v("ip"), [[0, 1]], 0, 1)
-    iota(v("i128"), [[0, 32], [-4, 4]], 128, 1)
+    iota(v("f128"), [[0, 32], [-4, 4]], 0, 0, True)
     iota(v("f24"), [[16, 24]], 128, 0, True)
     iota(v("ids"), [[4, C]], 0, 0, True)
     fill(v("half"), 0.5)
-    run("G", lambda: g.affine_select(v("ident")[0], v("half")[0], [[-1, 128]], Op.is_equal, 0.0, 0, 1), v("ident"), [v("half")])
-    fill(v("et"), 0.0)
+    select(v("ident"), v("half"), [[-1, 128]], Op.is_equal, 0, 1)
+    fill(v("bt", 0, 512), 0.0)
+    fill(v("reset"), 0.0)
+    fill(v("keep"), 1.0)
+    fill(v("mv", 0, HC), 0.0)
+    fill(v("mv", 13 * C, NF), 0.0)
     cp(v("uoff"), v("i8"))
-    ts(v("j384"), v("i384"), 15, Op.bitwise_and)
-    fill(v("base", 0, NV), 192.0)
-    fill(v("base", NV, 24), 384.0)
-    ts(v("sel"), v("j384"), 0.0, Op.is_equal)
-    ts(v("keep"), v("j384"), 0.0, Op.not_equal)
-    quant(v("qu"), v("su"), v("ut"))
-    cp((v("qur")[0].bitcast(dt.uint32), v("qur")[1]), ind(v("qu"), v("uoff"), True))
-    cp(v("sur"), ind(v("su"), v("uoff")))
-    ts(v("j128"), v("i128"), 15, Op.bitwise_and)
+    fill(v("reset", 0, HC, 16), FAR)
+    fill(v("keep", 0, C, 16), 0.0)
+    fill(v("pk"), 0.0)
+    fill(v("ovb", 24, 32), 0.0)
+    for j in range(4):
+        fill(v("w4", j, 192, 4), 4.0 ** (high[j - 1] - high[j]))
+    fill(v("w4", 0, 192, 8), 0.0)
+    for s in range(4):
+        act(v("bt", 5 * s, 512, 16), v("gb", s, 128, 4), Fn.Copy)
+    act(v("bt", 512, 1024), v("bt", 0, 512), Fn.Copy, scale=-1.0)
+    ts(v("j192"), v("i192"), 15, Op.bitwise_and)
     ts(v("jp", 0, 1), v("ip"), 15, Op.bitwise_and)
     ts(v("jp", 1, 2), v("ip"), 3, Op.bitwise_and)
-    ts(v("sel4"), v("j128"), 4.0, Op.is_lt)
-    quant(v("qx0"), v("sx0"), x0)
+    ts(v("far"), v("j192"), 0.0, Op.not_equal, 2 * FAR, Op.mult)
     cp(v("fp"), v("jp"))
-    ts(v("keep4"), v("j128"), 4.0, Op.is_ge)
-    ts(v("c128"), v("f24"), v("fp", 0, 1), Op.add)
-    fill(v("pk"), 0.0)
+    quant(v("qb"), v("sb"), v("bt"))
+    act(v("d128"), v("f128"), Fn.Identity, v("fp", 0, 1))
+    ts(v("ma"), v("d128"), 4.0, Op.is_ge, 2 * B, Op.mult)
+    ts(v("mb"), v("d128"), 0.0, Op.is_ge, B, Op.mult)
+    quant(v("qu"), v("su"), v("ut"))
+    tt(v("m4"), v("ma"), v("mb"), Op.subtract)
+    cp((v("qur")[0].bitcast(dt.uint32), v("qur")[1]), ind(v("qu"), v("uoff"), True))
+    pick_scales(v("sur"), ind(v("su"), v("uoff")))
+    quant(v("qx0"), v("sx0"), x0)
+    act(v("m96"), v("m4", 0, 96), Fn.Copy)
+    ts(v("cm", 0, 12), v("m4", 3, 48, 4), v("fp", 0, 1), Op.add, 2 * B + 192, Op.add)
+    ts(v("cm", 12, 24), v("m4", 3, 48, 4), v("fp", 0, 1), Op.add, 2 * B + 176, Op.add)
+    ts(v("m4", 3, 128, 4), v("m4", 3, 128, 4), v("fp", 1, 2), Op.add, 2 * B, Op.add)
 
     def half_tile(b):
         return v("qe", 128 * b, 128 * b + 128), v("se", 128 * b, 128 * b + 128)
 
     def offsets(name, src, b):
-        ts(v(name, 24 * b, 24 * b + 24), v(src), 4.0, Op.mult, float(b), Op.add)
+        ts(v(name, 24 * b, 24 * b + 24), v(src), 4.0, Op.mult, b - 4 * B, Op.add)
+
+    def where(k):
+        return (12 * C - 368 * k - 192, 192) if k < 12 else (12 * C - 368 * (k - 11), 176)
+
+    def level(k):
+        return v("tb", 16 * k + 15, 16 * k + 16)
 
     def sign(k):
-        j = k - NV
-        act(v("ms", j * C, j * C + C), v("cat", 16 * k + 16, 16 * k + 400), Fn.Sign, v("tb", 16 * k + 15, 16 * k + 16), -1.0)
+        act(v("ms", (k - 12) * 176, (k - 11) * 176), v("cat", 16 * k + 16, 16 * k + 192), Fn.Sign, level(k), -1.0)
 
-    def lost(k):
-        j = k - NV
-        act(v("ms", j * C, j * C + C), v("ms", j * C, j * C + C), Fn.Relu, acc=v("lc", j, j + 1))
+    def beats(k):
+        a, n = where(k)
+        act(v("mv", a, a + n), v("ms", (k - 12) * 176, (k - 11) * 176), Fn.Relu, acc=v("lc", k - 12, k - 11))
 
     def compare(k):
-        ts(v("mv", k * C, k * C + C), v("cat", 16 * k + 16, 16 * k + 400), v("tb", 16 * k + 15, 16 * k + 16), Op.is_ge)
+        a, n = where(k)
+        ts(v("mv", a, a + n), v("cat", 16 * k + 192 - n, 16 * k + 192), level(k), Op.is_lt)
 
     def total(k):
-        scan(v("sc", k * 192, k * 192 + 192), v("mv", k * C, k * C + 192), v("mv", k * C + 192, k * C + C), -192.0, Op.add, Op.add)
+        a, n = where(k)
+        h = n // 2
+        scan(v("sc", 96 * k + 96 - h, 96 * k + 96), v("mv", a, a + h), v("mv", a + h, a + n), 0.0, Op.add, Op.add)
+
+    def piece(n):
+        a, b = PIECES[n]
+        s = 0 if a == 0 else 32
+        quant(v("qm", a + s, b + s), v("sm", a + s, b + s), v("mv", 4 * a, 4 * b))
+        for q in range(12, -1, -1):
+            if a <= 96 * q < b and (a or q == 0):
+                o, c = 128 if q == 12 else 0, 96 * q + s
+                mm(6, 128, v("qb", o, o + 128), v("sb", o, o + 128), v("qm", c, c + 128), v("sm", c, c + 128), q == 12, q == 0)
 
     for t in range(R):
         win = "win%d" % t
@@ -253,66 +301,122 @@ def rank_program(g, core, T, topo):
         mean = 128 if t == 0 else 512
         wide = 768 if t == 0 else 1536
 
-        mm(4, C, v("qur"), v("sur"), qx, sx)
-        mm(5, C, v("qur"), v("sur"), qx, sx)
+        for bank, o in ((4, HC), (5, HC), (6, 0), (7, 0)):
+            mm(bank, HC, v("qur"), v("sur"), v("qx%d" % t, o, o + HC), v("sx%d" % t, o, o + HC))
         if t:
             send(peers[t], v("lqx%d" % t), qx, "ax%d" % t, True)
             send(peers[t], v("lsx%d" % t), sx, "ax%d" % t)
-        act(v("ab"), v("ps5", 0, C), Fn.Abs, 2.0 ** -124, 1.25 * 2.0 ** -24)
-        act(v("cat", C, 2 * C), v("ps5", 0, C), Fn.Copy)
-        tt(v("pm"), v("ps4", 0, C), v("sel"), Op.mult)
-        scan(v("tb"), v("keep"), v("pm"), 0.0, Op.mult, Op.add)
-        tt(v("cat", 0, C), v("ps4", 0, C), v("ab"), Op.subtract)
-        tt(v("eq"), v("ps4", 0, C), v("tb"), Op.is_equal)
+        act(v("ab"), v("ps5", 0, HC), Fn.Abs, 2.0 ** -124, 1.25 * 2.0 ** -24)
+        act(v("cat", HC, C), v("ps6", 0, HC), Fn.Copy)
+        for bank, o in ((4, HC), (7, 0)):
+            tt(v("pm", o, o + HC), v("ps%d" % bank, 0, HC), v("far"), Op.add)
+            scan(v("tb", o, o + HC), v("reset"), v("pm", o, o + HC), 0.0, Op.add, Op.min)
+        tt(v("cat", 0, HC), v("ps4", 0, HC), v("ab"), Op.subtract)
+        for bank, o in ((4, HC), (7, 0)):
+            tt(v("mv", 12 * C + o, 12 * C + o + HC), v("ps%d" % bank, 0, HC), v("tb", o, o + HC), Op.is_gt)
+        ks = list(range(12 + NHV, 24))
+        kv = list(range(12, 12 + NHV)) + list(range(12))
+        kv = sorted(kv, key=lambda k: -where(k)[0])
+        done = set()
+
+        def upto(a):
+            for k in ks:
+                if k not in done and sum(where(k)) > a:
+                    if k == ks[0]:
+                        sign(k)
+                        act(v("cat", C, C + 176), v("ps5", 0, 176), Fn.Copy)
+                    if k < 23:
+                        sign(k + 1)
+                    beats(k)
+                    done.add(k)
+
+        n = 0
+        for j, k in enumerate(kv):
+            compare(k)
+            if j == 0:
+                scan(v("ds"), v("keep"), v("mv", 12 * C, 13 * C), 0.0, Op.mult, Op.add)
+            else:
+                total(kv[j - 1])
+            if j == 1:
+                tt(v("cc"), v("cm"), v("ds", 15, C, 16), Op.add)
+            if n < len(PIECES) - 1 and j and where(kv[j - 1])[0] <= 4 * PIECES[n][0]:
+                upto(4 * PIECES[n][0])
+                piece(n)
+                n += 1
+        while n < len(PIECES) - 1:
+            upto(4 * PIECES[n][0])
+            piece(n)
+            n += 1
+        upto(0)
+        total(kv[-1])
+        piece(n)
+        tt(v("m96", 3, 48 + 4 * NHV, 4), v("cc", 0, 12 + NHV), v("sc", 95, 96 * (12 + NHV), 96), Op.subtract)
+        tt(v("m96", 51 + 4 * NHV, 96, 4), v("cc", 12 + NHV, 24), v("lc", NHV, 12), Op.subtract)
+        scan(v("rs"), v("ps6", 0, 96), v("m96"), B, Op.min, Op.add)
+        rk = v("rs", 3, 96, 4)
+        place = v("cnt%d" % t, 0, 24)
+        ts(place, rk, -B, Op.add)
+        send(peers[t], v(lcnt), v("cnt%d" % t), "ac%d" % t)
+        scatter(v("inv"), place, v("ids"))
+        act(v("sw1"), rk, Fn.Sign, B + 127.5, -1.0)
+        act(v("t1"), rk, Fn.Identity, B - 1000.0 * (B + 127), 1000.0)
+        act(v("wq"), v("sw1"), Fn.Relu, scale=field(rank))
+
+        def double_x(b):
+            act(v(win, 4 * 640 + b, 4 * 1024, 4), v("ps%d" % b, 0, C), Fn.Copy, scale=2.0)
+
         if t:
             for b in range(4):
                 mm(b, C, *half_tile(b), v("lqx%d" % t), v("lsx%d" % t))
-        ks = list(range(23, NV - 1, -1))
-        sign(ks[0])
-        for a, b in zip(ks, ks[1:]):
-            sign(b)
-            lost(a)
-        lost(ks[-1])
-        compare(0)
-        scan(v("eqs"), v("keep"), v("eq"), 0.0, Op.mult, Op.add)
-        for k in range(1, NV):
-            compare(k)
-            total(k - 1)
-            if k == 1:
-                tt(v("cc"), v("base"), v("eqs", 15, C, 16), Op.subtract)
-        total(NV - 1)
-        if t:
-            for b in range(4):
-                act(v(win, 4 * 640 + b, 4 * 1024, 4), v("ps%d" % b, 0, C), Fn.Copy, scale=2.0)
-        tt(v("rank", NV, 24), v("cc", NV, 24), v("lc"), Op.subtract)
-        tt(v("rank", 0, NV), v("sc", 191, NV * 192, 192), v("cc", 0, NV), Op.add)
-        place = v("cnt%d" % t, 0, 24) if t else v("ranku")
-        cp(place, v("rank"))
-        if t:
-            send(peers[t], v(lcnt), v("cnt%d" % t), "ac%d" % t)
-        scatter(v("inv"), place, v("ids"))
-        tt(v("p4"), v("inv", 0, 128), v("sel4"), Op.mult)
-        scan(v("s4"), v("keep4"), v("p4"), 0.0, Op.mult, Op.add)
-        ts(v(msg, 0, 32), v("s4", 3, 128, 4), v("fp", 1, 2), Op.add)
+            for b in range(3):
+                double_x(b)
+        scan(v("s4"), v("inv", 0, 128), v("m4"), B, Op.min, Op.add)
+        ts(v(msg, 0, 32), v("s4", 3, 128, 4), -B, Op.add)
+        if t == 0:
+            send(peers[t], v(lmsg), v(msg), "am%d" % t)
 
         xs = v(win, 512, 2048)
-        act(v("zt", 256, 512), ind(xs, v(msg, 16, 32)), Fn.Copy)
-        cp(v("zt", 0, 256), ind(xs, v(msg, 0, 16)))
-        ts(v("t1"), v("rank"), -127.0, Op.add, 1000.0, Op.mult)
+        act(v("zt", ZS, 512), ind(xs, v(msg, ZS // 16, 32)), Fn.Copy)
+        if t:
+            double_x(3)
+        cp(v("zt", 0, ZS), ind(xs, v(msg, 0, ZS // 16)))
+        tt(v("t2"), v("t1"), rk, Op.max)
         quant(v("qz"), v("sz"), v("zt"))
+        if t == 0:
+            ts(v("c128"), v("f24"), v("fp", 0, 1), Op.add, B, Op.add)
         for b in range(4):
             mm(4 + b, A, v("qw", 128 * b, 128 * b + 128), v("sw", 128 * b, 128 * b + 128), v("qz"), v("sz"))
         for b in range(4):
             act(v("rr", 128 * b, 128 * b + 128), v("ps%d" % (4 + b), 0, A), Fn.Relu, scale=0.03125)
-        tt(v("t2"), v("t1"), v("rank"), Op.max)
-        ts(v("wq"), v("rank"), 128.0, Op.is_lt, field(rank), Op.mult)
         tt(v("own"), v("t2"), v("c128"), Op.min)
         tt(v("pk"), v("pk"), v("wq"), Op.add)
-        cp(v(msg, 32, 56), v("own"))
-        send(peers[t], v(lmsg), v(msg), "am%d" % t)
+        if t:
+            ts(v(msg, 32, 56), v("own"), -B, Op.add)
+            send(peers[t], v(lmsg), v(msg), "am%d" % t)
         offsets("xoff", "own", 1)
-        for b in range(4):
+        if t:
+            ts(v("gm", 0, 24), v(lcnt, 0, 24), 128.0, Op.is_lt, field(rank ^ STEP[t]), Op.mult)
+            cp(v("gm", 24, 48), v(lcnt, 24, 48))
+
+        def add(b):
             tt(v(win, b, 512, 4), v("rr", 128 * b, 128 * b + 128), v("zt", b, 512, 4), Op.add)
+
+        add(0)
+        if t:
+            tt(v("pp", 0, 24), v("gm", 0, 24), v("gm", 24, 48), Op.add)
+        add(1)
+        if t == 1:
+            ts(v("nwu"), v("pp", 0, 24), 0.0, Op.is_equal)
+        if t == 2:
+            tt(v("pp", 24, 48), v("pp", 0, 24), v("pk"), Op.subtract)
+        add(2)
+        if t == 2:
+            ts(v("dd", 48, 72), v("pp", 24, 48), -1.0, Op.mult, float(GUARD), Op.add)
+        add(3)
+        if t == 2:
+            ts(v("an", 24, 48), v("dd", 48, 72), GUARD, Op.bitwise_and)
+        if t == 1:
+            act(v("wr"), ind(v("tab"), v("nwu")), Fn.Copy)
         quant(v("qh%d" % t), v("sh%d" % t), v(win, 0, 512))
         send(peers[t], v("lqh%d" % t), v("qh%d" % t), "ah%d" % t, True)
         send(peers[t], v("lsh%d" % t), v("sh%d" % t), "ah%d" % t)
@@ -327,85 +431,76 @@ def rank_program(g, core, T, topo):
         def mean_x(b):
             tt(v(win, 4 * 1152 + b, 4 * 1536, 4), v("ps%d" % b, 0, C), v("xh", b, 4 * C, 4), Op.add)
 
+        def cut():
+            scan(v("pre"), v("wr"), v("wr"), 0.0, Op.add, Op.max)
+            act(v("sg", K, C), v("pre", K, C), Fn.Sign, K + 0.5, -1.0, v("acc"))
+
         halve(1, "S")
         if t == 0:
             for b in (0, 3, 2):
                 offsets("xoff", "own", b)
             halve(0, "V")
             halve(3, "S")
-            halve(2, "V")
+            fill(v("et"), 0.0)
+            halve(2, "S")
             act(v("oh"), ind(v("xh"), v(lmsg, 0, 32)), Fn.Copy)
             for b in range(4):
                 cp(v("et", 513 * b, 512 * b + 512, 4), v("ident"))
-            ts(v("a1"), v("own"), 128.0, Op.is_lt, float(mean), Op.mult)
-            ts(v("mf"), v(lmsg, 32, 56), 512.0, Op.add)
+            ts(v("a1"), v("own"), B + 128, Op.is_lt, float(mean), Op.mult)
+            ts(v("mf"), v(lcnt), 512.0 + B, Op.add)
             quant(v("qe"), v("se"), v("et"))
-            tt(v("a2"), v("a1"), v("own"), Op.subtract)
-            ts(v("recv"), v("mf"), 640.0, Op.is_lt)
-        else:
-            ts(v("gm", 0, 24), v(lcnt, 0, 24), 128.0, Op.is_lt, field(rank ^ STEP[t]), Op.mult)
-            cp(v("gm", 24, 48), v(lcnt, 24, 48))
-            offsets("xoff", "own", 2)
-            tt(v("pp", 0, 24), v("gm", 0, 24), v("gm", 24, 48), Op.add)
-            offsets("xoff", "own", 0)
-            if t == 1:
-                ts(v("nwu"), v("pp", 0, 24), 0.0, Op.is_equal)
-                ts(v("fl"), v("pp", 0, 24), 0.0, Op.is_equal)
-                ts(v("a1"), v("pk"), 0.0, Op.is_gt, float(mean), Op.mult)
-                offsets("xoff", "own", 3)
-            else:
-                tt(v("pp", 24, 48), v("pp", 0, 24), v("pk"), Op.subtract)
-                offsets("xoff", "own", 3)
-                ts(v("dd", 48, 72), v("pp", 24, 48), -1.0, Op.mult, float(GUARD), Op.add)
-                ts(v("dd", 24, 48), v("pp", 24, 48), float(GUARD), Op.add)
-                ts(v("an", 24, 48), v("dd", 48, 72), GUARD, Op.bitwise_and)
-                ts(v("an", 0, 24), v("dd", 24, 48), GUARD, Op.bitwise_and)
-                ts(v("nwu"), v("an", 24, 48), float(GUARD), Op.is_equal)
-                ts(v("fl"), v("an", 24, 48), float(GUARD), Op.is_equal)
-                ts(v("a1"), v("an", 0, 24), float(GUARD), Op.not_equal, float(mean), Op.mult)
-                halve(2, "S")
-            act(v("wr"), ind(v("tab"), v("nwu")), Fn.Copy)
-            if t == 1:
-                halve(0, "V")
-                halve(2, "S")
-            else:
-                halve(0, "S")
-                mean_x(1)
-                mean_x(2)
-            tt(v("a2"), v("a1"), v("own"), Op.subtract)
-            scan(v("pre"), v("wr"), v("wr"), 0.0, Op.add, Op.max)
-            act(v("sg", K, C), v("pre", K, C), Fn.Sign, K + 0.5, -1.0, v("acc"))
-            halve(3, "S")
-            act(v("oh"), ind(v("xh"), v(lmsg, 0, 32)), Fn.Copy)
-            if t == 1:
-                mean_x(1)
-            mean_x(0)
-            ts(v("cut"), v("c2"), v("acc"), Op.is_lt)
-            if t == 1:
-                mean_x(2)
-            ts(v("mf"), v(lmsg, 32, 56), 512.0, Op.add)
-            tt(v("recv"), v("cut"), v("fl"), Op.is_gt)
-        tt(v("b1"), v("mf"), v("a2"), Op.add)
-        if t:
-            mean_x(3)
-        else:
+            ts(v("want"), v(lcnt), 128.0, Op.is_lt, BB, Op.mult)
+            tt(v("b1"), v("mf"), v("a1"), Op.add)
             quant(v("qv"), v("sv"), v("vt"))
-        tt(v("d1"), v("b1"), v("recv"), Op.mult)
-        tt(v("src"), v("d1"), v("own"), Op.add)
+            tt(v("d1"), v("b1"), v("want"), Op.min)
+        else:
+            if t == 2:
+                ts(v("nwu"), v("an", 24, 48), float(GUARD), Op.is_equal)
+            offsets("xoff", "own", 3)
+            if t == 1:
+                cut()
+            else:
+                act(v("wr"), ind(v("tab"), v("nwu")), Fn.Copy)
+            offsets("xoff", "own", 0)
+            offsets("xoff", "own", 2)
+            halve(3, "S")
+            halve(0, "V")
+            if t == 1:
+                ts(v("a1"), v("pk"), 0.0, Op.is_gt, float(mean), Op.mult)
+                ts(v("want"), v("pp", 0, 24), 0.0, Op.is_gt, BB, Op.mult)
+            else:
+                cut()
+                ts(v("dd", 24, 48), v("pp", 24, 48), float(GUARD), Op.add)
+                ts(v("want"), v("an", 24, 48), float(GUARD), Op.not_equal, BB, Op.mult)
+                ts(v("an", 0, 24), v("dd", 24, 48), GUARD, Op.bitwise_and)
+            halve(2, "S")
+            act(v("oh"), ind(v("xh"), v(lmsg, 0, 32)), Fn.Copy)
+            mean_x(1)
+            if t == 2:
+                ts(v("a1"), v("an", 0, 24), float(GUARD), Op.not_equal, float(mean), Op.mult)
+            ts(v("mf"), v(lmsg, 32, 56), 512.0 + B, Op.add)
+            mean_x(0)
+            tt(v("b1"), v("mf"), v("a1"), Op.add)
+            ts(v("cut"), v("c2"), v("acc"), Op.is_lt, BB, Op.mult)
+            mean_x(3)
+            tt(v("recv"), v("cut"), v("want"), Op.min)
+            mean_x(2)
+            tt(v("d1"), v("b1"), v("recv"), Op.min)
+        tt(v("src"), v("d1"), v("own"), Op.max)
         for b in range(4):
             offsets("foff", "src", b)
         if t == 0:
-            ts(v("c2"), v("c128"), 2.0, Op.mult, -256.0 - (C + K), Op.add)
+            ts(v("c2"), v("c128"), 2.0, Op.mult, -2 * B - 256.0 - (C + K), Op.add)
             fill(v("tab", 0, 1), 1.0)
             fill(v("tab", 1, 16), 0.0)
+            ts(v("inc"), v(lcnt), 128.0, Op.is_lt, field(rank ^ STEP[0]), Op.mult)
 
         for b in range(4):
             mm(4 + b, A, *half_tile(b), v("lqh%d" % t), v("lsh%d" % t))
-            mm(b, A, *half_tile(b), v("lqh%d" % t), v("lsh%d" % t))
         for b in range(4):
-            act(v(win, 4 * 512 + b, 4 * 640, 4), v("ps%d" % b, 0, A), Fn.Copy, scale=2.0)
             o = 4 * (512 + mean)
             tt(v(win, o + b, o + 512, 4), v("ps%d" % (4 + b), 0, A), v("oh", b, 512, 4), Op.add)
+            act(v(win, 4 * 512 + b, 4 * 640, 4), v("ps%d" % (4 + b), 0, A), Fn.Copy, scale=2.0)
         nxt, o = ("win%d" % (t + 1), 512) if t < R - 1 else ("xlast", 0)
         for b in range(4):
             out, src = v(nxt, o + b, o + 4 * C, 4), ind(v(win, 0, 4 * wide), v("foff", 24 * b, 24 * b + 24))
@@ -415,14 +510,8 @@ def rank_program(g, core, T, topo):
                 cp(out, src)
         quant(v("qx%d" % (t + 1)), v("sx%d" % (t + 1)), v(nxt, o, o + 4 * C))
         if t < 2:
-            if t == 0:
-                ts(v("inc"), v("recv"), field(rank ^ STEP[0]), Op.mult)
-                fill(v("ovb", 24, 32), 0.0)
-                fill(v("w4", 1, 192, 2), 1.0)
-            else:
-                tt(v("inc"), v("cut"), v("pp", 0, 24), Op.mult)
-            for j in (2 * t, 2 * t + 1):
-                fill(v("w4", 2 * j, 192, 8), float(4 ** (high[j - 1] - high[j])) if j else 0.0)
+            if t:
+                tt(v("inc"), v("cut"), v("pp", 0, 24), Op.min)
             tt(v("pk"), v("pk"), v("inc"), Op.add)
             cp(v("cnt%d" % (t + 1), 24, 48), v("pk"))
 
@@ -433,12 +522,10 @@ def rank_program(g, core, T, topo):
         dma("Y", T.osc[4 * k:4 * k + 4, :], T["sx%d" % R][32 * k:32 * k + 4, :], "outy", reads=sx[1])
     act(v("ysb"), v("ps4", 0, C), Fn.Copy)
     dma("S", T.y[:], v("ysb")[0], "outs", reads=v("ysb")[1])
-    tt(v("inc"), v("pp", 24, 48), v("recv"), Op.mult)
-    ts(v("dd", 0, 48, 2), v("pk"), float(GUARD), Op.add)
-    ts(v("dd", 1, 48, 2), v("inc"), float(GUARD), Op.add)
+    ts(v("de", 0, 48, 2), v("pk"), float(GUARD), Op.add)
+    tt(v("de", 1, 48, 2), v("dd", 24, 48), v("recv"), Op.min)
     for j in range(4):
-        for h in range(2):
-            ts(v("un", 2 * j + h, 192, 8), v("dd", h, 48, 2), 4 * coset.index(high[j] ^ first), Op.logical_shift_right, 7, Op.bitwise_and)
+        ts(v("un", j, 192, 4), v("de"), 4 * coset.index(high[j] ^ first), Op.logical_shift_right, 7, Op.bitwise_and)
     ts(v("uf"), v("un"), -4.0, Op.add, 0.0, Op.max)
     scan(v("ug"), v("w4"), v("uf"), 0.0, Op.mult, Op.add)
     ts(v("ovb", 0, 24), v("ug", 7, 192, 8), float(4 ** high[3]), Op.mult)

@@ -2,15 +2,28 @@ from concourse.mybir import dt, AluOpType, ActivationFunctionType
 
 STEP = [2, 5, 7]
 C, A, K, R = 384, 128, 160, 3
-HC = C // 2
+LO = 160
+HI = C - LO
 GUARD = 0x4444
 FAR = 1e28
 B = 4096.0
 BB = 65536.0
 NF = 5120
-PIECES = [(828, 1280), (552, 828), (276, 552), (96, 276), (0, 128)]
-NHV = 0
-ZS = 256
+PIECES = [(1152, 1280, [12]), (0, 416, [0, 1, 2, 3]), (416, 704, [4, 5, 6]), (704, 896, [7, 8]),
+          (896, 1056, [9, 10]), (1056, 1184, [11])]
+AFTER = [9, 6, 3, 1, 1, -1]
+KS = list(range(23, 12, -1)) + [0, 12]
+KV = list(range(11, 0, -1))
+DH = "SSSS"
+NS = 1
+ZS = [256, 256, 256]
+E1, E2 = [0, 0, 0], [5, 11, 16]
+OV = 192
+UPPER = [("V", 0, 0, 14), ("S", 1, 0, 14), ("V", 2, 0, 14), ("S", 3, 0, 14)]
+LOWER = [("V", 0, 0, 10), ("S", 1, 0, 10), ("S", 2, 0, 10), ("S", 3, 0, 10)]
+LAST = LOWER
+BANKS = (6, 7)
+DX3 = True
 Q4 = "float8_e4m3fn_x4"
 
 
@@ -24,22 +37,22 @@ SCRATCH = {
     "xh": _sb(4 * C, BF), "zt": _sb(512, BF), "oh": _sb(512, BF), "rr": _sb(512), "ut": _sb(512, BF), "vt": _sb(512, BF),
     "qu": _sb(128, Q4), "su": _sb(128, U8), "qur": _sb(128, Q4), "sur": _sb(128, U8), "qv": _sb(128, Q4), "sv": _sb(128, U8),
     "qw": _sb(512, Q4), "sw": _sb(512, U8), "qe": _sb(512, Q4), "se": _sb(512, U8), "qz": _sb(128, Q4), "sz": _sb(128, U8),
-    "et": _sb(2048, BF), "half": _sb(128, BF), "ident": _sb(128, BF),
+    "et": _sb(1032, BF), "zero": _sb(516, BF), "ppk": _sb(48),
+    "oa": _sb(48), "ob": _sb(48), "sa": _sb(96), "sb4": _sb(96), "so": _sb(96),
     "ones": _sb(128, BF), "gb1": _sb(128, BF), "gb": _sb(128, BF), "bt": _sb(1024, BF), "qb": _sb(256, Q4), "sb": _sb(256, U8),
-    "i8": _sb(8, I32), "uoff": _sb(8, U16), "i192": _sb(HC, I32), "j192": _sb(HC, I32), "f128": _sb(128), "d128": _sb(128),
-    "ip": _sb(1, I32), "jp": _sb(2, I32), "far": _sb(HC), "reset": _sb(HC), "keep": _sb(C, BF),
-    "ma": _sb(128), "mb": _sb(128), "m4": _sb(128), "m96": _sb(96), "ids": _sb(C), "w4": _sb(192), "tab": _sb(16, BF),
-    "cat": _sb(560), "ab": _sb(HC), "pm": _sb(C), "tb": _sb(C), "ds": _sb(C, BF),
-    "mv": _sb(NF, BF), "qm": _sb(NF // 4 + 32, Q4), "sm": _sb(NF // 4 + 32, U8), "sc": _sb(24 * 96, BF), "ms": _sb(12 * 176, BF),
+    "i8": _sb(8, I32), "uoff": _sb(8, U16), "f192": _sb(HI), "f4": _sb(4), "d4": _sb(4),
+    "ip": _sb(1, I32), "jp": _sb(2, I32), "far": _sb(HI), "reset": _sb(HI), "keep": _sb(C, BF),
+    "ma": _sb(4), "mb": _sb(4), "mc": _sb(6), "m4": _sb(128), "m96": _sb(96), "ids": _sb(C), "w4": _sb(192), "tab": _sb(16, BF),
+    "cat": _sb(560), "ab": _sb(176), "pm": _sb(C), "tb": _sb(C), "ds": _sb(C, BF),
+    "mv": _sb(NF, BF), "qm": _sb(NF // 4 + 128, Q4), "sm": _sb(NF // 4 + 128, U8), "sc": _sb(12 * 96, BF), "ms": _sb(12 * C, BF),
     "rs": _sb(96), "inv": _sb(C), "s4": _sb(128),
-    "xoff": _sb(96, U16), "foff": _sb(96, U16), "dd": _sb(72, I32), "de": _sb(48, I32), "an": _sb(48, I32), "nwu": _sb(24, U16),
+    "xoff": _sb(96, U16), "foff": _sb(96, U16), "dd": _sb(48, I32), "de": _sb(48, I32), "an": _sb(48, I32), "nwu": _sb(24, U16),
     "wr": _sb(C, BF), "pre": _sb(C, BF), "sg": _sb(C, BF),
     "un": _sb(192, I32), "uf": _sb(192), "ug": _sb(192), "ovb": _sb(32), "ovt": _sb(32), "ysb": _sb(C),
 }
 SMALL = {}
-for _n, _w in (("fp", 2), ("acc", 1), ("gm", 48), ("pp", 48), ("lc", 12)) + tuple((_k, 24) for _k in (
-        "f24", "c128", "c2", "cm", "cc", "t1", "t2", "sw1", "own", "wq", "pk", "want", "mf", "a1", "b1", "b2", "cut",
-        "recv", "d1", "src", "inc")):
+for _n, _w in (("fp", 2), ("acc", 1), ("gm", 48), ("df", 24), ("lc", 24)) + tuple((_k, 24) for _k in (
+        "f24", "c2", "cm", "cc", "sw1", "wq", "recv", "inc")):
     SMALL[_n] = (48 * len(SMALL), _w)
 SCRATCH["small"] = _sb(48 * len(SMALL))
 for _t in range(R + 1):
@@ -54,7 +67,7 @@ for _t in (1, 2):
 for _b in range(8):
     SCRATCH["ps%d" % _b] = ("psum", [128, 512], "float32")
 
-SEMAPHORES = ["V", "S", "P", "G", "ldx", "ldu", "ldv", "ldw", "sent", "outy", "outs",
+SEMAPHORES = ["V", "S", "P", "G", "ldx", "ldz", "ldu", "ldv", "ldw", "sent", "outy", "outs",
               "ah0", "ah1", "ah2", "am0", "am1", "am2", "ax1", "ax2", "ac0", "ac1", "ac2"]
 
 
@@ -169,8 +182,8 @@ def rank_program(g, core, T, topo):
         else:
             run("G", lambda: g.iota(out[0], pattern, base, mult), out, [])
 
-    def select(out, in_, pattern, op, base, mult):
-        run("G", lambda: g.affine_select(out[0], in_[0], pattern, op, 0.0, base, mult), out, [in_])
+    def select(out, in_, pattern, op, base, mult, other=0.0):
+        run("G", lambda: g.affine_select(out[0], in_[0], pattern, op, other, base, mult), out, [in_])
 
     def dma(q, out, in_, sem, reads=(), writes=(), last=None):
         before(q, list(reads), list(writes))
@@ -199,82 +212,95 @@ def rank_program(g, core, T, topo):
         lands(peers[t], ["lmsg%d" % t], "am%d" % t)
         lands(peers[t], ["lcnt%d" % t], "ac%d" % t)
         if t:
-            lands(peers[t], ["lqx%d" % t, "lsx%d" % t], "ax%d" % t)
+            lands(peers[t], ["lqx%d" % t, "lqx%d" % t, "lsx%d" % t], "ax%d" % t)
 
     def field(r):
         return float(16 ** coset.index(r ^ first))
 
     x0 = v("win0", 512, 2048)
     dma("Y", v("ut")[0], T.u[:], "ldu", writes=v("ut")[1])
-    dma("S", x0[0], T.x[:], "ldx", writes=x0[1])
+    upper_x, lower_x = v("win0", 512 + 4 * LO, 2048), v("win0", 512, 512 + 4 * LO)
+    dma("Y", upper_x[0], T.x[:, 4 * LO:], "ldx", writes=upper_x[1])
+    fill(v("ones"), 1.0)
+    iota(v("i8"), [[16, 8]], 0, 0)
+    iota(v("ip"), [[0, 1]], 0, 1)
+    iota(v("f192"), [[0, HI // 16], [1, 16]], 0, 0, True)
+    select(v("gb1"), v("ones"), [[-16, 8], [0, 16]], Op.is_ge, 0, 1)
+    iota(v("f4"), [[-4, 4]], 0, 0, True)
+    select(v("gb"), v("gb1"), [[16, 8], [0, 16]], Op.is_ge, 15, -1)
+    iota(v("f24"), [[16, 24]], 128 + int(B), 0, True)
+    iota(v("ids"), [[4, C]], 0, 0, True)
+    iota(v("zero"), [[0, 516]], 0, 0, True)
+    for h in range(2):
+        select(v("et", 516 * h, 516 * h + 516), v("zero"), [[-1, 129], [1000, 4]], Op.not_equal, -1000 * (2 + h), 1, 0.5)
+    pk, pp = v("ppk", 0, 24), v("ppk", 24, 48)
+    fill(v("bt", 0, 512), 0.0)
+    cp(v("uoff"), v("i8"))
+    for a, b in ((10 * C, 11 * C + 128), (12 * C - 192, 12 * C), (13 * C, NF)):
+        fill(v("mv", a, b), 0.0)
+    quant(v("qm", 960, 1088), v("sm", 960, 1088), v("mv", 10 * C, 11 * C + 128))
+    ts(v("jp", 0, 1), v("ip"), 15, Op.bitwise_and)
+    ts(v("jp", 1, 2), v("ip"), 3, Op.bitwise_and)
+    fill(pk, 0.0)
+    cp(v("fp"), v("jp"))
+    act(v("reset"), v("f192"), Fn.Relu, FAR, -FAR)
+    dma("S", lower_x[0], T.x[:, :4 * LO], "ldz", writes=lower_x[1])
     before("Y", x0[1], [])
     dma("Y", v("qw")[0].bitcast(dt.uint8), T.wc[:], "ldw", writes=v("qw")[1], last=32)
     dma("Y", v("sw")[0], T.ws[:], "ldw", writes=v("sw")[1], last=32)
     dma("Y", v("vt")[0], T.v[:], "ldv", writes=v("vt")[1])
-    fill(v("ones"), 1.0)
-    iota(v("i8"), [[16, 8]], 0, 0)
-    select(v("gb1"), v("ones"), [[-16, 8], [0, 16]], Op.is_ge, 0, 1)
-    select(v("gb"), v("gb1"), [[16, 8], [0, 16]], Op.is_ge, 15, -1)
-    iota(v("i192"), [[0, 12], [1, 16]], 128, -1)
-    iota(v("ip"), [[0, 1]], 0, 1)
-    iota(v("f128"), [[0, 32], [-4, 4]], 0, 0, True)
-    iota(v("f24"), [[16, 24]], 128, 0, True)
-    iota(v("ids"), [[4, C]], 0, 0, True)
-    fill(v("half"), 0.5)
-    select(v("ident"), v("half"), [[-1, 128]], Op.is_equal, 0, 1)
-    fill(v("bt", 0, 512), 0.0)
-    fill(v("reset"), 0.0)
-    fill(v("keep"), 1.0)
-    fill(v("mv", 0, HC), 0.0)
-    fill(v("mv", 13 * C, NF), 0.0)
-    cp(v("uoff"), v("i8"))
-    fill(v("reset", 0, HC, 16), FAR)
-    fill(v("keep", 0, C, 16), 0.0)
-    fill(v("pk"), 0.0)
-    fill(v("ovb", 24, 32), 0.0)
-    for j in range(4):
-        fill(v("w4", j, 192, 4), 4.0 ** (high[j - 1] - high[j]))
-    fill(v("w4", 0, 192, 8), 0.0)
+    for o in (0, 192):
+        act(v("keep", o, o + 192), v("f192", 0, 192), Fn.Sign)
+    ts(v("far"), v("f192"), v("fp", 0, 1), Op.not_equal, 2 * FAR, Op.mult)
+    quant(v("qu"), v("su"), v("ut"))
+    ts(v("d4"), v("f4"), v("fp", 0, 1), Op.add)
+    cp((v("qur")[0].bitcast(dt.uint32), v("qur")[1]), ind(v("qu"), v("uoff"), True))
+    pick_scales(v("sur"), ind(v("su"), v("uoff")))
+    ts(v("ma"), v("d4"), 4.0, Op.is_ge, 2 * B, Op.mult)
+    ts(v("mb"), v("d4"), 0.0, Op.is_ge, B, Op.mult)
     for s in range(4):
         act(v("bt", 5 * s, 512, 16), v("gb", s, 128, 4), Fn.Copy)
     act(v("bt", 512, 1024), v("bt", 0, 512), Fn.Copy, scale=-1.0)
-    ts(v("j192"), v("i192"), 15, Op.bitwise_and)
-    ts(v("jp", 0, 1), v("ip"), 15, Op.bitwise_and)
-    ts(v("jp", 1, 2), v("ip"), 3, Op.bitwise_and)
-    ts(v("far"), v("j192"), 0.0, Op.not_equal, 2 * FAR, Op.mult)
-    cp(v("fp"), v("jp"))
-    quant(v("qb"), v("sb"), v("bt"))
-    act(v("d128"), v("f128"), Fn.Identity, v("fp", 0, 1))
-    ts(v("ma"), v("d128"), 4.0, Op.is_ge, 2 * B, Op.mult)
-    ts(v("mb"), v("d128"), 0.0, Op.is_ge, B, Op.mult)
-    quant(v("qu"), v("su"), v("ut"))
-    tt(v("m4"), v("ma"), v("mb"), Op.subtract)
-    cp((v("qur")[0].bitcast(dt.uint32), v("qur")[1]), ind(v("qu"), v("uoff"), True))
-    pick_scales(v("sur"), ind(v("su"), v("uoff")))
-    quant(v("qx0"), v("sx0"), x0)
-    act(v("m96"), v("m4", 0, 96), Fn.Copy)
-    ts(v("cm", 0, 12), v("m4", 3, 48, 4), v("fp", 0, 1), Op.add, 2 * B + 192, Op.add)
-    ts(v("cm", 12, 24), v("m4", 3, 48, 4), v("fp", 0, 1), Op.add, 2 * B + 176, Op.add)
-    ts(v("m4", 3, 128, 4), v("m4", 3, 128, 4), v("fp", 1, 2), Op.add, 2 * B, Op.add)
+
+    def selectors():
+        tt(v("mc", 0, 4), v("ma"), v("mb"), Op.subtract)
+        spread("m96", 96, range(3))
+        for h, n in enumerate((176, 192)):
+            ts(v("cm", h, h + 1), v("mc", 3, 4), v("fp", 0, 1), Op.add, 2 * B + n, Op.add)
+
+    def const(out, c):
+        act(out, v("f192", 0, bin(out[1][0][1]).count("1")), Fn.Identity, c, 0.0)
+
+    def spread(name, n, cs):
+        for c in cs:
+            ts(v(name, c, n, 4), v("f192", 0, n // 4), 0.0, Op.mult, v("mc", c, c + 1), Op.add)
+
+    def constants():
+        fill(v("tab", 0, 1), 1.0)
+        fill(v("tab", 1, 16), 0.0)
+        fill(v("ovb", 24, 32), 0.0)
+        fill(v("w4", 4, 192, 8), 4.0 ** (high[3] - high[0]))
+        fill(v("w4", 0, 192, 8), 0.0)
 
     def half_tile(b):
         return v("qe", 128 * b, 128 * b + 128), v("se", 128 * b, 128 * b + 128)
 
     def offsets(name, src, b):
-        ts(v(name, 24 * b, 24 * b + 24), v(src), 4.0, Op.mult, b - 4 * B, Op.add)
+        ts(v(name, 24 * b, 24 * b + 24), src, 4.0, Op.mult, b - 4 * B, Op.add)
 
     def where(k):
-        return (12 * C - 368 * k - 192, 192) if k < 12 else (12 * C - 368 * (k - 11), 176)
+        return (368 * (11 - k), 176) if k < 12 else (368 * (23 - k) + 176, 192)
 
     def level(k):
         return v("tb", 16 * k + 15, 16 * k + 16)
 
     def sign(k):
-        act(v("ms", (k - 12) * 176, (k - 11) * 176), v("cat", 16 * k + 16, 16 * k + 192), Fn.Sign, level(k), -1.0)
+        a, n = where(k)
+        act(v("ms", a, a + n), v("cat", 16 * k + 192 - n, 16 * k + 192), Fn.Sign, level(k), -1.0)
 
     def beats(k):
         a, n = where(k)
-        act(v("mv", a, a + n), v("ms", (k - 12) * 176, (k - 11) * 176), Fn.Relu, acc=v("lc", k - 12, k - 11))
+        act(v("mv", a, a + n), v("ms", a, a + n), Fn.Relu, acc=v("lc", k, k + 1))
 
     def compare(k):
         a, n = where(k)
@@ -286,13 +312,28 @@ def rank_program(g, core, T, topo):
         scan(v("sc", 96 * k + 96 - h, 96 * k + 96), v("mv", a, a + h), v("mv", a + h, a + n), 0.0, Op.add, Op.add)
 
     def piece(n):
-        a, b = PIECES[n]
-        s = 0 if a == 0 else 32
+        a, b, rows = PIECES[n]
+        s = 224 if rows == [11] else 0
         quant(v("qm", a + s, b + s), v("sm", a + s, b + s), v("mv", 4 * a, 4 * b))
-        for q in range(12, -1, -1):
-            if a <= 96 * q < b and (a or q == 0):
-                o, c = 128 if q == 12 else 0, 96 * q + s
-                mm(6, 128, v("qb", o, o + 128), v("sb", o, o + 128), v("qm", c, c + 128), v("sm", c, c + 128), q == 12, q == 0)
+        for q in rows:
+            o, c = 128 if q == 12 else 0, 96 * q + s
+            mm(6, 128, v("qb", o, o + 128), v("sb", o, o + 128), v("qm", c, c + 128), v("sm", c, c + 128), q == 12, q == 11)
+
+    end = {LO: C, 0: LO}
+
+    def state(t, o, who, meanwhile=None):
+        nxt, a = ("win%d" % t, 512 + 4 * o) if t < R else ("xlast", 4 * o)
+        for q, b, lo, hi in who if t else []:
+            f = 24 * b + o // 16
+            out = v(nxt, a + 64 * lo + b, a + 64 * hi, 4)
+            src = ind(v("win%d" % (t - 1), 0, 4 * (768 if t == 1 else 1536)), v("foff", f + lo, f + hi))
+            if q == "S":
+                act(out, src, Fn.Copy)
+            else:
+                cp(out, src)
+        if meanwhile:
+            meanwhile()
+        quant(v("qx%d" % t, o, end[o]), v("sx%d" % t, o, end[o]), v(nxt, a, a + 4 * (end[o] - o)))
 
     for t in range(R):
         win = "win%d" % t
@@ -301,57 +342,91 @@ def rank_program(g, core, T, topo):
         mean = 128 if t == 0 else 512
         wide = 768 if t == 0 else 1536
 
-        for bank, o in ((4, HC), (5, HC), (6, 0), (7, 0)):
-            mm(bank, HC, v("qur"), v("sur"), v("qx%d" % t, o, o + HC), v("sx%d" % t, o, o + HC))
+        def scores(bank, o):
+            mm(bank, end[o] - o, v("qur"), v("sur"), v("qx%d" % t, o, end[o]), v("sx%d" % t, o, end[o]))
+
+        def masked(bank, o):
+            tt(v("pm", o, end[o]), v("ps%d" % bank, 0, end[o] - o), v("far", 0, end[o] - o), Op.add)
+
+        def levels(o):
+            scan(v("tb", o, end[o]), v("reset", 0, end[o] - o), v("pm", o, end[o]), 0.0, Op.add, Op.min)
+
+        def within(bank, o):
+            tt(v("mv", 12 * C + o, 12 * C + end[o]), v("ps%d" % bank, 0, end[o] - o), v("tb", o, end[o]), Op.is_gt)
+
+        state(t, LO, UPPER)
+        scores(4, LO)
+        scores(5, LO)
         if t:
-            send(peers[t], v("lqx%d" % t), qx, "ax%d" % t, True)
+            send(peers[t], v("lqx%d" % t, LO, C), v("qx%d" % t, LO, C), "ax%d" % t, True)
+        if t == 0:
+            selectors()
+        def upper():
+            masked(4, LO)
+            if t == 2:
+                tt(v("inc"), v("sa", 2, 96, 4), pp, Op.min)
+            levels(LO)
+
+        state(t, 0, LOWER, upper)
+        for bank in BANKS:
+            scores(bank, 0)
+        if t:
+            send(peers[t], v("lqx%d" % t, 0, LO), v("qx%d" % t, 0, LO), "ax%d" % t, True)
             send(peers[t], v("lsx%d" % t), sx, "ax%d" % t)
-        act(v("ab"), v("ps5", 0, HC), Fn.Abs, 2.0 ** -124, 1.25 * 2.0 ** -24)
-        act(v("cat", HC, C), v("ps6", 0, HC), Fn.Copy)
-        for bank, o in ((4, HC), (7, 0)):
-            tt(v("pm", o, o + HC), v("ps%d" % bank, 0, HC), v("far"), Op.add)
-            scan(v("tb", o, o + HC), v("reset"), v("pm", o, o + HC), 0.0, Op.add, Op.min)
-        tt(v("cat", 0, HC), v("ps4", 0, HC), v("ab"), Op.subtract)
-        for bank, o in ((4, HC), (7, 0)):
-            tt(v("mv", 12 * C + o, 12 * C + o + HC), v("ps%d" % bank, 0, HC), v("tb", o, o + HC), Op.is_gt)
-        ks = list(range(12 + NHV, 24))
-        kv = list(range(12, 12 + NHV)) + list(range(12))
-        kv = sorted(kv, key=lambda k: -where(k)[0])
-        done = set()
+        act(v("ab"), v("ps5", HI - 176, HI), Fn.Abs, 2.0 ** -124, 1.25 * 2.0 ** -24)
+        act(v("cat", 192 + LO, 560), v("ps5", 0, 368 - LO), Fn.Copy)
+        sign(23)
+        sign(22)
+        beats(23)
+        act(v("cat", 192, 192 + LO), v("ps6", 0, LO), Fn.Copy)
+        within(4, LO)
+        tt(v("cat", 16, 192), v("ps4", HI - 176, HI), v("ab"), Op.subtract)
+        if t == 0:
+            quant(v("qb"), v("sb"), v("bt"))
+        masked(7, 0)
+        if t == 2:
+            tt(pk, pk, v("inc"), Op.add)
+        levels(0)
+        ks, kv = KS, KV
+        done = [23]
 
         def upto(a):
-            for k in ks:
-                if k not in done and sum(where(k)) > a:
-                    if k == ks[0]:
-                        sign(k)
-                        act(v("cat", C, C + 176), v("ps5", 0, 176), Fn.Copy)
-                    if k < 23:
-                        sign(k + 1)
-                    beats(k)
-                    done.add(k)
+            while any(where(k)[0] < a for k in ks[len(done):]):
+                j = len(done)
+                if j + 1 < len(ks):
+                    sign(ks[j + 1])
+                beats(ks[j])
+                done.append(ks[j])
 
         n = 0
         for j, k in enumerate(kv):
             compare(k)
             if j == 0:
-                scan(v("ds"), v("keep"), v("mv", 12 * C, 13 * C), 0.0, Op.mult, Op.add)
+                within(7, 0)
             else:
                 total(kv[j - 1])
             if j == 1:
-                tt(v("cc"), v("cm"), v("ds", 15, C, 16), Op.add)
-            if n < len(PIECES) - 1 and j and where(kv[j - 1])[0] <= 4 * PIECES[n][0]:
-                upto(4 * PIECES[n][0])
+                scan(v("ds"), v("keep"), v("mv", 12 * C, 13 * C), 0.0, Op.mult, Op.add)
+            while k == AFTER[n]:
+                if n:
+                    upto(4 * PIECES[n][1])
                 piece(n)
                 n += 1
-        while n < len(PIECES) - 1:
-            upto(4 * PIECES[n][0])
-            piece(n)
-            n += 1
-        upto(0)
+        upto(NF)
+        for h in range(2):
+            act(v("cc", 12 * h, 12 * h + 12), v("ds", 192 * h + 15, 192 * h + 192, 16), Fn.Identity, v("cm", h, h + 1))
         total(kv[-1])
         piece(n)
-        tt(v("m96", 3, 48 + 4 * NHV, 4), v("cc", 0, 12 + NHV), v("sc", 95, 96 * (12 + NHV), 96), Op.subtract)
-        tt(v("m96", 51 + 4 * NHV, 96, 4), v("cc", 12 + NHV, 24), v("lc", NHV, 12), Op.subtract)
+        a, b = min(kv), max(kv) + 1
+        tt(v("m96", 3 + 4 * a, 4 * b, 4), v("cc", a, b), v("sc", 95 + 96 * a, 96 * b, 96), Op.subtract)
+        for a, b in ((0, a), (b, 24)):
+            if a < b:
+                tt(v("m96", 3 + 4 * a, 4 * b, 4), v("cc", a, b), v("lc", a, b), Op.subtract)
+        if t == 0:
+            ts(v("mc", 4, 5), v("mc", 3, 4), v("fp", 1, 2), Op.add, 2 * B, Op.add)
+            spread("m4", 128, range(1))
+        if t == 2:
+            cp(v("cnt2", 24, 48), pk)
         scan(v("rs"), v("ps6", 0, 96), v("m96"), B, Op.min, Op.add)
         rk = v("rs", 3, 96, 4)
         place = v("cnt%d" % t, 0, 24)
@@ -359,64 +434,78 @@ def rank_program(g, core, T, topo):
         send(peers[t], v(lcnt), v("cnt%d" % t), "ac%d" % t)
         scatter(v("inv"), place, v("ids"))
         act(v("sw1"), rk, Fn.Sign, B + 127.5, -1.0)
-        act(v("t1"), rk, Fn.Identity, B - 1000.0 * (B + 127), 1000.0)
+        act(v("oa", 1, 48, 2), rk, Fn.Identity, B - 1000.0 * (B + 127), 1000.0)
+        act(v("ob", 0, 48, 2), rk, Fn.Copy)
         act(v("wq"), v("sw1"), Fn.Relu, scale=field(rank))
+        own = v("sb4", 3, 96, 4)
+        if t == 0:
+            for c in (1, 2, 3):
+                act(v("m4", c, 128, 4), v("f192", 0, 32), Fn.Identity, v("mc", c + c // 3, c + c // 3 + 1), 0.0)
+            act(v("ob", 1, 48, 2), v("f24"), Fn.Identity, v("fp", 0, 1))
+            const(v("oa", 0, 48, 2), BB)
 
         def double_x(b):
             act(v(win, 4 * 640 + b, 4 * 1024, 4), v("ps%d" % b, 0, C), Fn.Copy, scale=2.0)
 
         if t:
-            for b in range(4):
-                mm(b, C, *half_tile(b), v("lqx%d" % t), v("lsx%d" % t))
             for b in range(3):
+                mm(b, C, *half_tile(b), v("lqx%d" % t), v("lsx%d" % t))
                 double_x(b)
+        scan(v("sb4", 1, 96, 2), v("oa"), v("ob"), 0.0, Op.max, Op.min)
         scan(v("s4"), v("inv", 0, 128), v("m4"), B, Op.min, Op.add)
+        if t:
+            ts(v(msg, 32, 56), own, -B, Op.add)
         ts(v(msg, 0, 32), v("s4", 3, 128, 4), -B, Op.add)
-        if t == 0:
-            send(peers[t], v(lmsg), v(msg), "am%d" % t)
+        send(peers[t], v(lmsg), v(msg), "am%d" % t)
 
         xs = v(win, 512, 2048)
-        act(v("zt", ZS, 512), ind(xs, v(msg, ZS // 16, 32)), Fn.Copy)
+        act(v("zt", ZS[t], 512), ind(xs, v(msg, ZS[t] // 16, 32)), Fn.Copy)
         if t:
+            mm(3, C, *half_tile(3), v("lqx%d" % t), v("lsx%d" % t))
             double_x(3)
-        cp(v("zt", 0, ZS), ind(xs, v(msg, 0, ZS // 16)))
-        tt(v("t2"), v("t1"), rk, Op.max)
-        quant(v("qz"), v("sz"), v("zt"))
+        cp(v("zt", 0, ZS[t]), ind(xs, v(msg, 0, ZS[t] // 16)))
+        early = []
+        if t:
+            early += [lambda: ts(v("gm", 0, 24), v(lcnt, 0, 24), 128.0, Op.is_lt, field(rank ^ STEP[t]), Op.mult),
+                      lambda: ts(v("gm", 24, 48), v(lcnt, 24, 48), -float(GUARD) * (t - 1), Op.add),
+                      lambda: tt(pk, pk, v("wq"), Op.add),
+                      lambda: tt(pp, v("gm", 0, 24), v("gm", 24, 48), Op.add),
+                      lambda: offsets("xoff", own, 1)]
+        if t == 1:
+            early += [lambda: ts(v("nwu"), pp, 0.0, Op.is_equal)]
+        if t == 2:
+            early += [lambda: tt(v("dd", 24, 48), pk, pp, Op.subtract),
+                      lambda: offsets("xoff", own, 3),
+                      lambda: ts(v("an", 24, 48), v("dd", 24, 48), GUARD, Op.bitwise_and),
+                      lambda: offsets("xoff", own, 0),
+                      lambda: ts(v("nwu"), v("an", 24, 48), float(GUARD), Op.is_equal)]
         if t == 0:
-            ts(v("c128"), v("f24"), v("fp", 0, 1), Op.add, B, Op.add)
+            early += [lambda b=b: offsets("xoff", own, b) for b in (1, 3, 0, 2)] + [lambda: tt(pk, pk, v("wq"), Op.add)]
+            early += [lambda: [fill(v(name, a, 96, 4), c) for name, a, c in (("sa", 0, -BB), ("sb4", 2, -BB), ("sa", 2, BB))]]
+        for call in early[:E1[t]]:
+            call()
+        quant(v("qz"), v("sz"), v("zt"))
         for b in range(4):
             mm(4 + b, A, v("qw", 128 * b, 128 * b + 128), v("sw", 128 * b, 128 * b + 128), v("qz"), v("sz"))
         for b in range(4):
-            act(v("rr", 128 * b, 128 * b + 128), v("ps%d" % (4 + b), 0, A), Fn.Relu, scale=0.03125)
-        tt(v("own"), v("t2"), v("c128"), Op.min)
-        tt(v("pk"), v("pk"), v("wq"), Op.add)
-        if t:
-            ts(v(msg, 32, 56), v("own"), -B, Op.add)
-            send(peers[t], v(lmsg), v(msg), "am%d" % t)
-        offsets("xoff", "own", 1)
-        if t:
-            ts(v("gm", 0, 24), v(lcnt, 0, 24), 128.0, Op.is_lt, field(rank ^ STEP[t]), Op.mult)
-            cp(v("gm", 24, 48), v(lcnt, 24, 48))
+            act(v("rr", b, 512, 4), v("ps%d" % (4 + b), 0, A), Fn.Relu, scale=0.03125)
+        for call in early[E1[t]:E2[t]]:
+            call()
+        late = early[E2[t]:]
 
-        def add(b):
-            tt(v(win, b, 512, 4), v("rr", 128 * b, 128 * b + 128), v("zt", b, 512, 4), Op.add)
-
-        add(0)
-        if t:
-            tt(v("pp", 0, 24), v("gm", 0, 24), v("gm", 24, 48), Op.add)
-        add(1)
-        if t == 1:
-            ts(v("nwu"), v("pp", 0, 24), 0.0, Op.is_equal)
-        if t == 2:
-            tt(v("pp", 24, 48), v("pp", 0, 24), v("pk"), Op.subtract)
-        add(2)
-        if t == 2:
-            ts(v("dd", 48, 72), v("pp", 24, 48), -1.0, Op.mult, float(GUARD), Op.add)
-        add(3)
-        if t == 2:
-            ts(v("an", 24, 48), v("dd", 48, 72), GUARD, Op.bitwise_and)
-        if t == 1:
+        def wanted():
             act(v("wr"), ind(v("tab"), v("nwu")), Fn.Copy)
+
+        both, far_mean, far_d, cut_at, want = v("sb4", 0, 96, 4), v("sa", 1, 96, 4), v("sb4", 1, 96, 4), v("sa", 2, 96, 4), v("sa", 3, 96, 4)
+        if t == 0:
+            act(both, v("sw1"), Fn.Relu, scale=BB)
+            act(v("c2"), v("ob", 1, 48, 2), Fn.Identity, -2 * B - 256.0 - (C + K), 2.0)
+            for j in range(3):
+                const(v("w4", j + 1, 192, 4), 4.0 ** (high[j] - high[j + 1]))
+        if t:
+            wanted()
+        for b in range(4):
+            tt(v(win, b, 512, 4), v("rr", b, 512, 4), v("zt", b, 512, 4), Op.add)
         quant(v("qh%d" % t), v("sh%d" % t), v(win, 0, 512))
         send(peers[t], v("lqh%d" % t), v("qh%d" % t), "ah%d" % t, True)
         send(peers[t], v("lsh%d" % t), v("sh%d" % t), "ah%d" % t)
@@ -437,101 +526,100 @@ def rank_program(g, core, T, topo):
 
         halve(1, "S")
         if t == 0:
-            for b in (0, 3, 2):
-                offsets("xoff", "own", b)
+            for call in late:
+                call()
             halve(0, "V")
             halve(3, "S")
-            fill(v("et"), 0.0)
-            halve(2, "S")
+            halve(2, "V")
             act(v("oh"), ind(v("xh"), v(lmsg, 0, 32)), Fn.Copy)
+            ts(far_d, v(lcnt), 512.0 + B, Op.add)
+            ts(far_mean, v(lcnt), 512.0 + B + mean, Op.add)
+            ts(want, v(lcnt), 128.0, Op.is_lt, BB, Op.mult)
             for b in range(4):
-                cp(v("et", 513 * b, 512 * b + 512, 4), v("ident"))
-            ts(v("a1"), v("own"), B + 128, Op.is_lt, float(mean), Op.mult)
-            ts(v("mf"), v(lcnt), 512.0 + B, Op.add)
-            quant(v("qe"), v("se"), v("et"))
-            ts(v("want"), v(lcnt), 128.0, Op.is_lt, BB, Op.mult)
-            tt(v("b1"), v("mf"), v("a1"), Op.add)
+                o = 516 * (b % 2) + 2 - b // 2 * 2
+                quant(*half_tile(b), v("et", o, o + 512))
+                if b == 0:
+                    scan(v("so"), v("sa"), v("sb4"), 0.0, Op.min, Op.max)
             quant(v("qv"), v("sv"), v("vt"))
-            tt(v("d1"), v("b1"), v("want"), Op.min)
-        else:
-            if t == 2:
-                ts(v("nwu"), v("an", 24, 48), float(GUARD), Op.is_equal)
-            offsets("xoff", "own", 3)
-            if t == 1:
-                cut()
-            else:
-                act(v("wr"), ind(v("tab"), v("nwu")), Fn.Copy)
-            offsets("xoff", "own", 0)
-            offsets("xoff", "own", 2)
-            halve(3, "S")
-            halve(0, "V")
-            if t == 1:
-                ts(v("a1"), v("pk"), 0.0, Op.is_gt, float(mean), Op.mult)
-                ts(v("want"), v("pp", 0, 24), 0.0, Op.is_gt, BB, Op.mult)
-            else:
-                cut()
-                ts(v("dd", 24, 48), v("pp", 24, 48), float(GUARD), Op.add)
-                ts(v("want"), v("an", 24, 48), float(GUARD), Op.not_equal, BB, Op.mult)
-                ts(v("an", 0, 24), v("dd", 24, 48), GUARD, Op.bitwise_and)
-            halve(2, "S")
-            act(v("oh"), ind(v("xh"), v(lmsg, 0, 32)), Fn.Copy)
-            mean_x(1)
-            if t == 2:
-                ts(v("a1"), v("an", 0, 24), float(GUARD), Op.not_equal, float(mean), Op.mult)
-            ts(v("mf"), v(lmsg, 32, 56), 512.0 + B, Op.add)
-            mean_x(0)
-            tt(v("b1"), v("mf"), v("a1"), Op.add)
-            ts(v("cut"), v("c2"), v("acc"), Op.is_lt, BB, Op.mult)
-            mean_x(3)
-            tt(v("recv"), v("cut"), v("want"), Op.min)
-            mean_x(2)
-            tt(v("d1"), v("b1"), v("recv"), Op.min)
-        tt(v("src"), v("d1"), v("own"), Op.max)
-        for b in range(4):
-            offsets("foff", "src", b)
-        if t == 0:
-            ts(v("c2"), v("c128"), 2.0, Op.mult, -2 * B - 256.0 - (C + K), Op.add)
-            fill(v("tab", 0, 1), 1.0)
-            fill(v("tab", 1, 16), 0.0)
             ts(v("inc"), v(lcnt), 128.0, Op.is_lt, field(rank ^ STEP[0]), Op.mult)
+        else:
+            for b in (0, 3)[:2 * (2 - t)]:
+                offsets("xoff", own, b)
+            cut()
+            offsets("xoff", own, 2)
+            if t == 2:
+                ts(v("dd", 0, 24), v("dd", 24, 48), -1.0, Op.mult, 2.0 * GUARD, Op.add)
+            halve(0, "V")
+            halve(3, "S")
+            halve(2, "S")
+            act(v("oh", OV, 512), ind(v("xh"), v(lmsg, OV // 16, 32)), Fn.Copy)
+            if t == 1:
+                ts(both, pk, BB, Op.mult)
+                ts(want, pp, BB, Op.mult)
+            if t == 2:
+                ts(v("an", 0, 24), v("dd", 0, 24), GUARD, Op.bitwise_and)
+                ts(want, v("an", 24, 48), float(GUARD), Op.not_equal, BB, Op.mult)
+            ts(far_d, v(lmsg, 32, 56), 512.0 + B, Op.add)
+            mean_x(1)
+            ts(far_mean, v(lmsg, 32, 56), 512.0 + B + mean, Op.add)
+            ts(cut_at, v("c2"), v("acc"), Op.is_lt, BB, Op.mult)
+            if t == 2:
+                ts(both, v("an", 0, 24), float(GUARD), Op.not_equal, BB, Op.mult)
+            mean_x(0)
+            scan(v("so"), v("sa"), v("sb4"), 0.0, Op.min, Op.max)
+            mean_x(3)
+            if t == 2:
+                tt(v("recv"), cut_at, want, Op.min)
+        for b in range(4):
+            offsets("foff", v("so", 3, 96, 4), b)
+        if t:
+            mean_x(2)
+            cp(v("oh", 0, OV), ind(v("xh"), v(lmsg, 0, OV // 16)))
+        if t == 0:
+            tt(pk, pk, v("inc"), Op.add)
+            constants()
+            cp(v("cnt1", 24, 48), pk)
+
 
         for b in range(4):
             mm(4 + b, A, *half_tile(b), v("lqh%d" % t), v("lsh%d" % t))
         for b in range(4):
             o = 4 * (512 + mean)
-            tt(v(win, o + b, o + 512, 4), v("ps%d" % (4 + b), 0, A), v("oh", b, 512, 4), Op.add)
-            act(v(win, 4 * 512 + b, 4 * 640, 4), v("ps%d" % (4 + b), 0, A), Fn.Copy, scale=2.0)
-        nxt, o = ("win%d" % (t + 1), 512) if t < R - 1 else ("xlast", 0)
-        for b in range(4):
-            out, src = v(nxt, o + b, o + 4 * C, 4), ind(v(win, 0, 4 * wide), v("foff", 24 * b, 24 * b + 24))
-            if b % 2:
-                act(out, src, Fn.Copy)
-            else:
-                cp(out, src)
-        quant(v("qx%d" % (t + 1)), v("sx%d" % (t + 1)), v(nxt, o, o + 4 * C))
-        if t < 2:
-            if t:
-                tt(v("inc"), v("cut"), v("pp", 0, 24), Op.min)
-            tt(v("pk"), v("pk"), v("inc"), Op.add)
-            cp(v("cnt%d" % (t + 1), 24, 48), v("pk"))
+            whole, halves = v(win, 4 * 512 + b, 4 * 640, 4), v("ps%d" % (4 + b), 0, A)
+            if DH[b] == "S":
+                act(whole, halves, Fn.Copy, scale=2.0)
+            tt(v(win, o + b, o + 512, 4), halves, v("oh", b, 512, 4), Op.add)
+            if DH[b] == "s":
+                act(whole, halves, Fn.Copy, scale=2.0)
+            if DH[b] == "v":
+                ts(whole, halves, 2.0, Op.mult)
 
     qx, sx = v("qx%d" % R), v("sx%d" % R)
-    mm(4, C, v("qv"), v("sv"), qx, sx)
+
+    def fields():
+        for j in range(4):
+            ts(v("un", j, 192, 4), v("de"), 4 * coset.index(high[j] ^ first), Op.logical_shift_right, 7, Op.bitwise_and)
+        ts(v("uf"), v("un"), -4.0, Op.add, 0.0, Op.max)
+
+    def pairs():
+        tt(v("de", 1, 48, 2), v("dd", 0, 24), v("recv"), Op.min)
+        ts(v("de", 0, 48, 2), pk, float(GUARD), Op.add)
+
+    for bank, o, who, meanwhile in ((4, LO, UPPER, pairs), (5, 0, LAST, fields)):
+        state(R, o, who, meanwhile)
+        mm(bank, end[o] - o, v("qv"), v("sv"), v("qx%d" % R, o, end[o]), v("sx%d" % R, o, end[o]))
+    act(v("ysb", LO, C), v("ps4", 0, HI), Fn.Copy)
     dma("Y", T.oc[:], qx[0].bitcast(dt.uint8), "outy", reads=qx[1])
-    for k in range(4):
-        dma("Y", T.osc[4 * k:4 * k + 4, :], T["sx%d" % R][32 * k:32 * k + 4, :], "outy", reads=sx[1])
-    act(v("ysb"), v("ps4", 0, C), Fn.Copy)
+    act(v("ysb", 0, LO), v("ps5", 0, LO), Fn.Copy)
     dma("S", T.y[:], v("ysb")[0], "outs", reads=v("ysb")[1])
-    ts(v("de", 0, 48, 2), v("pk"), float(GUARD), Op.add)
-    tt(v("de", 1, 48, 2), v("dd", 24, 48), v("recv"), Op.min)
-    for j in range(4):
-        ts(v("un", j, 192, 4), v("de"), 4 * coset.index(high[j] ^ first), Op.logical_shift_right, 7, Op.bitwise_and)
-    ts(v("uf"), v("un"), -4.0, Op.add, 0.0, Op.max)
+    for k in range(4):
+        q, sem = ("S", "outs") if k == 3 else ("Y", "outy")
+        dma(q, T.osc[4 * k:4 * k + 4, :], T["sx%d" % R][32 * k:32 * k + 4, :], sem, reads=sx[1])
     scan(v("ug"), v("w4"), v("uf"), 0.0, Op.mult, Op.add)
     ts(v("ovb", 0, 24), v("ug", 7, 192, 8), float(4 ** high[3]), Op.mult)
     run("V", lambda: g.vector.transpose(v("ovt")[0], v("ovb")[0]), v("ovt"), [v("ovb")])
     for k in range(8):
-        q, sem = ("Y", "outy") if k % 2 else ("S", "outs")
+        q, sem = ("S", "outs") if k % 2 else ("Y", "outy")
         a, h = k // 2, k % 2
         dma(q, T.ov[k:k + 1, :], T["ovt"][32 * a:32 * a + 24, 16 * h:16 * h + 16], sem, reads=v("ovt")[1])
     wait("G", "G", count["G"])

from concourse.mybir import dt, AluOpType, ActivationFunctionType

STEP = [2, 5, 7]
C, A, K, R = 384, 128, 160, 3
LO = 160
HI = C - LO
GUARD = 0x4444
FAR = 1e28
B = 4096.0
BB = 65536.0
NF = 5120
PIECES = [(1152, 1280, [12]), (0, 416, [0, 1, 2, 3]), (416, 704, [4, 5, 6]), (704, 896, [7, 8]),
          (896, 1056, [9, 10]), (1056, 1184, [11])]
AFTER = [9, 6, 3, 1, 1, -1]
KS = list(range(23, 12, -1)) + [0, 12]
KV = list(range(11, 0, -1))
DH = "SSSS"
NS = 1
ZS = [256, 256, 256]
E1, E2 = [0, 0, 0], [5, 11, 16]
OV = 192
UPPER = [("V", 0, 0, 14), ("S", 1, 0, 14), ("V", 2, 0, 14), ("S", 3, 0, 14)]
LOWER = [("V", 0, 0, 10), ("S", 1, 0, 10), ("S", 2, 0, 10), ("S", 3, 0, 10)]
LAST = LOWER
BANKS = (6, 7)
DX3 = True
Q4 = "float8_e4m3fn_x4"


def _sb(n, d="float32"):
    return ("sbuf", [128, n], d)


BF, I32, U16, U8 = "bfloat16", "int32", "uint16", "uint8"
SCRATCH = {
    "win0": _sb(4 * 768, BF), "win1": _sb(4 * 1536, BF), "win2": _sb(4 * 1536, BF), "xlast": _sb(4 * C, BF),
    "xh": _sb(4 * C, BF), "zt": _sb(512, BF), "oh": _sb(512, BF), "rr": _sb(512), "ut": _sb(512, BF), "vt": _sb(512, BF),
    "qu": _sb(128, Q4), "su": _sb(128, U8), "qur": _sb(128, Q4), "sur": _sb(128, U8), "qv": _sb(128, Q4), "sv": _sb(128, U8),
    "qw": _sb(512, Q4), "sw": _sb(512, U8), "qe": _sb(512, Q4), "se": _sb(512, U8), "qz": _sb(128, Q4), "sz": _sb(128, U8),
    "et": _sb(1032, BF), "zero": _sb(516, BF), "ppk": _sb(48),
    "oa": _sb(48), "ob": _sb(48), "sa": _sb(96), "sb4": _sb(96), "so": _sb(96),
    "ones": _sb(128, BF), "gb1": _sb(128, BF), "gb": _sb(128, BF), "bt": _sb(1024, BF), "qb": _sb(256, Q4), "sb": _sb(256, U8),
    "i8": _sb(8, I32), "uoff": _sb(8, U16), "f192": _sb(HI), "f4": _sb(4), "d4": _sb(4),
    "ip": _sb(1, I32), "jp": _sb(2, I32), "far": _sb(HI), "reset": _sb(HI), "keep": _sb(C, BF),
    "ma": _sb(4), "mb": _sb(4), "mc": _sb(6), "m4": _sb(128), "m96": _sb(96), "ids": _sb(C), "w4": _sb(192), "tab": _sb(16, BF),
    "cat": _sb(560), "ab": _sb(176), "pm": _sb(C), "tb": _sb(C), "ds": _sb(C, BF),
    "mv": _sb(NF, BF), "qm": _sb(NF // 4 + 128, Q4), "sm": _sb(NF // 4 + 128, U8), "sc": _sb(12 * 96, BF), "ms": _sb(12 * C, BF),
    "rs": _sb(96), "inv": _sb(C), "s4": _sb(128),
    "xoff": _sb(96, U16), "foff": _sb(96, U16), "dd": _sb(48, I32), "de": _sb(48, I32), "an": _sb(48, I32), "nwu": _sb(24, U16),
    "wr": _sb(C, BF), "pre": _sb(C, BF), "sg": _sb(C, BF),
    "un": _sb(192, I32), "uf": _sb(192), "ug": _sb(192), "ovb": _sb(32), "ovt": _sb(32), "ysb": _sb(C),
}
SMALL = {}
for _n, _w in (("fp", 2), ("acc", 1), ("gm", 48), ("df", 24), ("lc", 24)) + tuple((_k, 24) for _k in (
        "f24", "c2", "cm", "cc", "sw1", "wq", "recv", "inc")):
    SMALL[_n] = (48 * len(SMALL), _w)
SCRATCH["small"] = _sb(48 * len(SMALL))
for _t in range(R + 1):
    SCRATCH["qx%d" % _t], SCRATCH["sx%d" % _t] = _sb(C, Q4), _sb(C, U8)
for _t in range(R):
    SCRATCH["qh%d" % _t], SCRATCH["sh%d" % _t] = _sb(A, Q4), _sb(A, U8)
    SCRATCH["lqh%d" % _t], SCRATCH["lsh%d" % _t] = _sb(A, Q4), _sb(A, U8)
    SCRATCH["msg%d" % _t] = SCRATCH["lmsg%d" % _t] = _sb(56 if _t else 32, U16)
    SCRATCH["cnt%d" % _t] = SCRATCH["lcnt%d" % _t] = _sb(48 if _t else 24, U16)
for _t in (1, 2):
    SCRATCH["lqx%d" % _t], SCRATCH["lsx%d" % _t] = _sb(C, Q4), _sb(C, U8)
for _b in range(8):
    SCRATCH["ps%d" % _b] = ("psum", [128, 512], "float32")

SEMAPHORES = ["V", "S", "P", "G", "ldx", "ldz", "ldu", "ldv", "ldw", "sent", "outy", "outs",
              "ah0", "ah1", "ah2", "am0", "am1", "am2", "ax1", "ax2", "ac0", "ac1", "ac2"]


def rank_program(g, core, T, topo):
    rank = T.rank_of(core)
    if rank is None:
        return
    Op, Fn = AluOpType, ActivationFunctionType
    queues = {"V": g.vector, "S": g.scalar, "P": g.tensor, "G": g, "Y": g.sync}
    known = {q: {} for q in queues}
    count = {}
    seen = {}

    def v(name, a=None, b=None, s=None):
        if name in SMALL:
            r = range(SMALL[name][0], sum(SMALL[name]))[a:b:s]
            name = "small"
        else:
            r = range(T[name].shape[1])[a:b:s]
        t = T[name]
        if name.startswith("ps"):
            m = 1
        elif r.step == 1:
            m = ((1 << len(r)) - 1) << r.start
        else:
            m = sum(1 << i for i in r)
        ap = t[:, r.start:r.stop] if r.step == 1 else t[:, r.start:r.stop:r.step]
        return (ap, [(name, m)])

    def ind(win, off, words=False):
        ap = win[0].bitcast(dt.uint32) if words else win[0]
        return (ap.indirect(off[0]), win[1] + off[1])

    def wait(q, sem, val, clock=None):
        if known[q].get(sem, 0) < val:
            queues[q].wait_ge(T.sem[sem], val)
            known[q][sem] = val
        for s, n in (clock or {}).items():
            if known[q].get(s, 0) < n:
                known[q][s] = n

    def before(q, reads, writes, adds=False):
        need = []
        for acc, wr in ((reads, False), (writes, True)):
            for name, m in acc:
                for e in seen.get(name, []):
                    if e[0] & m and (wr or e[1] or (name.startswith("ps") and e[2] != q)) and not (adds and wr and e[2] == q):
                        need.append(e)
        for e in sorted(need, key=lambda e: -e[4]):
            wait(q, e[3], e[4], e[5])

    def after(q, reads, writes, sem, val):
        clock = dict(known[q])
        for name, m in writes:
            seen[name] = [e for e in seen.get(name, []) if e[0] & ~m] + [[m, True, q, sem, val, clock]]
        for name, m in reads:
            seen.setdefault(name, []).append([m, False, q, sem, val, clock])

    def run(q, call, out, ins, also=None, adds=False):
        reads = [x for i in ins if isinstance(i, tuple) for x in i[1]]
        writes = list(out[1]) + (list(also[1]) if also else [])
        before(q, reads, writes, adds)
        count[q] = count.get(q, 0) + 1
        call().then_inc(T.sem[q], 1)
        after(q, reads, writes, q, count[q])

    def ap(x):
        return x[0] if isinstance(x, tuple) else x

    def cp(out, in_):
        run("V", lambda: g.vector.tensor_copy(out[0], in_[0]), out, [in_])

    def scatter(win, off, in_):
        run("V", lambda: g.vector.tensor_copy(win[0].indirect(off[0]), in_[0]), win, [off, in_])

    def tt(out, a, b, op):
        run("V", lambda: g.vector.tensor_tensor(out[0], a[0], b[0], op), out, [a, b])

    def ts(out, a, s1, op0, s2=None, op1=None):
        if op1 is None:
            run("V", lambda: g.vector.tensor_scalar(out[0], a[0], ap(s1), None, op0), out, [a, s1])
        else:
            run("V", lambda: g.vector.tensor_scalar(out[0], a[0], ap(s1), ap(s2), op0, op1), out, [a, s1, s2])

    def scan(out, d0, d1, init, op0, op1):
        run("V", lambda: g.vector.tensor_tensor_scan(out[0], d0[0], d1[0], init, op0, op1), out, [d0, d1])

    def fill(out, c):
        run("V", lambda: g.vector.memset(out[0], c), out, [])

    def quant(q, s, in_):
        run("V", lambda: g.vector.quantize_mx(q[0], s[0], in_[0]), q, [in_], s)

    def act(out, in_, fn, bias=None, scale=1.0, acc=None):
        kw = {"scale": scale}
        if bias is not None:
            kw["bias"] = ap(bias)
        if acc is not None:
            kw["accum_out"] = acc[0]
        run("S", lambda: g.scalar.activation(out[0], in_[0], fn, **kw), out, [in_, bias], acc)

    def pick_scales(out, in_):
        run("S", lambda: g.scalar.activation(out[0], in_[0], Fn.Copy), out, [in_])

    def mm(bank, n, lq, ls, rq, rs, start=True, stop=True):
        out = v("ps%d" % bank, 0, n)
        run("P", lambda: g.tensor.matmul_mx(out[0], lq[0], ls[0], rq[0], rs[0], start, stop), out, [lq, ls, rq, rs], adds=not start)

    def iota(out, pattern, base, mult, real=False):
        if real:
            run("G", lambda: g.iota(out[0], pattern, base, mult, allow_small_or_imprecise_dtypes=True), out, [])
        else:
            run("G", lambda: g.iota(out[0], pattern, base, mult), out, [])

    def select(out, in_, pattern, op, base, mult, other=0.0):
        run("G", lambda: g.affine_select(out[0], in_[0], pattern, op, other, base, mult), out, [in_])

    def dma(q, out, in_, sem, reads=(), writes=(), last=None):
        before(q, list(reads), list(writes))
        count[sem] = count.get(sem, 0) + 16
        queues[q].dma_start(out, in_).then_inc(T.sem[sem], 16)
        after(q, list(reads), list(writes), sem, last or count[sem])

    def send(peer, dst, src, sem, codes=False):
        before("G", src[1], [])
        rid, pid, _ = topo.addr(peer)
        o, i = (dst[0].bitcast(dt.uint8), src[0].bitcast(dt.uint8)) if codes else (dst[0], src[0])
        g.remote_dma(o, i, T.sem[sem], T.sem["sent"], pid, rid, topo.mask(core, peer))
        count["sent"] = count.get("sent", 0) + len(topo.engines(core, peer))

    def lands(peer, names, sem):
        n = len(names) * len(topo.engines(peer, core))
        for name in names:
            seen[name] = [[v(name)[1][0][1], True, None, sem, n, {}]]

    peers = [T.cores[rank ^ s] for s in STEP]
    coset = [0] + STEP
    first = min(rank ^ d for d in coset)
    high = sorted((rank ^ d for d in coset), reverse=True)
    for t in range(R):
        lands(peers[t], ["lqh%d" % t, "lsh%d" % t], "ah%d" % t)
        lands(peers[t], ["lmsg%d" % t], "am%d" % t)
        lands(peers[t], ["lcnt%d" % t], "ac%d" % t)
        if t:
            lands(peers[t], ["lqx%d" % t, "lqx%d" % t, "lsx%d" % t], "ax%d" % t)

    def field(r):
        return float(16 ** coset.index(r ^ first))

    x0 = v("win0", 512, 2048)
    dma("Y", v("ut")[0], T.u[:], "ldu", writes=v("ut")[1])
    upper_x, lower_x = v("win0", 512 + 4 * LO, 2048), v("win0", 512, 512 + 4 * LO)
    dma("Y", upper_x[0], T.x[:, 4 * LO:], "ldx", writes=upper_x[1])
    fill(v("ones"), 1.0)
    iota(v("i8"), [[16, 8]], 0, 0)
    iota(v("ip"), [[0, 1]], 0, 1)
    iota(v("f192"), [[0, HI // 16], [1, 16]], 0, 0, True)
    select(v("gb1"), v("ones"), [[-16, 8], [0, 16]], Op.is_ge, 0, 1)
    iota(v("f4"), [[-4, 4]], 0, 0, True)
    select(v("gb"), v("gb1"), [[16, 8], [0, 16]], Op.is_ge, 15, -1)
    iota(v("f24"), [[16, 24]], 128 + int(B), 0, True)
    iota(v("ids"), [[4, C]], 0, 0, True)
    iota(v("zero"), [[0, 516]], 0, 0, True)
    for h in range(2):
        select(v("et", 516 * h, 516 * h + 516), v("zero"), [[-1, 129], [1000, 4]], Op.not_equal, -1000 * (2 + h), 1, 0.5)
    pk, pp = v("ppk", 0, 24), v("ppk", 24, 48)
    fill(v("bt", 0, 512), 0.0)
    cp(v("uoff"), v("i8"))
    for a, b in ((10 * C, 11 * C + 128), (12 * C - 192, 12 * C), (13 * C, NF)):
        fill(v("mv", a, b), 0.0)
    quant(v("qm", 960, 1088), v("sm", 960, 1088), v("mv", 10 * C, 11 * C + 128))
    ts(v("jp", 0, 1), v("ip"), 15, Op.bitwise_and)
    ts(v("jp", 1, 2), v("ip"), 3, Op.bitwise_and)
    fill(pk, 0.0)
    cp(v("fp"), v("jp"))
    act(v("reset"), v("f192"), Fn.Relu, FAR, -FAR)
    dma("S", lower_x[0], T.x[:, :4 * LO], "ldz", writes=lower_x[1])
    before("Y", x0[1], [])
    dma("Y", v("qw")[0].bitcast(dt.uint8), T.wc[:], "ldw", writes=v("qw")[1], last=32)
    dma("Y", v("sw")[0], T.ws[:], "ldw", writes=v("sw")[1], last=32)
    dma("Y", v("vt")[0], T.v[:], "ldv", writes=v("vt")[1])
    for o in (0, 192):
        act(v("keep", o, o + 192), v("f192", 0, 192), Fn.Sign)
    ts(v("far"), v("f192"), v("fp", 0, 1), Op.not_equal, 2 * FAR, Op.mult)
    quant(v("qu"), v("su"), v("ut"))
    ts(v("d4"), v("f4"), v("fp", 0, 1), Op.add)
    cp((v("qur")[0].bitcast(dt.uint32), v("qur")[1]), ind(v("qu"), v("uoff"), True))
    pick_scales(v("sur"), ind(v("su"), v("uoff")))
    ts(v("ma"), v("d4"), 4.0, Op.is_ge, 2 * B, Op.mult)
    ts(v("mb"), v("d4"), 0.0, Op.is_ge, B, Op.mult)
    for s in range(4):
        act(v("bt", 5 * s, 512, 16), v("gb", s, 128, 4), Fn.Copy)
    act(v("bt", 512, 1024), v("bt", 0, 512), Fn.Copy, scale=-1.0)

    def selectors():
        tt(v("mc", 0, 4), v("ma"), v("mb"), Op.subtract)
        spread("m96", 96, range(3))
        for h, n in enumerate((176, 192)):
            ts(v("cm", h, h + 1), v("mc", 3, 4), v("fp", 0, 1), Op.add, 2 * B + n, Op.add)

    def const(out, c):
        act(out, v("f192", 0, bin(out[1][0][1]).count("1")), Fn.Identity, c, 0.0)

    def spread(name, n, cs):
        for c in cs:
            ts(v(name, c, n, 4), v("f192", 0, n // 4), 0.0, Op.mult, v("mc", c, c + 1), Op.add)

    def constants():
        fill(v("tab", 0, 1), 1.0)
        fill(v("tab", 1, 16), 0.0)
        fill(v("ovb", 24, 32), 0.0)
        fill(v("w4", 4, 192, 8), 4.0 ** (high[3] - high[0]))
        fill(v("w4", 0, 192, 8), 0.0)

    def half_tile(b):
        return v("qe", 128 * b, 128 * b + 128), v("se", 128 * b, 128 * b + 128)

    def offsets(name, src, b):
        ts(v(name, 24 * b, 24 * b + 24), src, 4.0, Op.mult, b - 4 * B, Op.add)

    def where(k):
        return (368 * (11 - k), 176) if k < 12 else (368 * (23 - k) + 176, 192)

    def level(k):
        return v("tb", 16 * k + 15, 16 * k + 16)

    def sign(k):
        a, n = where(k)
        act(v("ms", a, a + n), v("cat", 16 * k + 192 - n, 16 * k + 192), Fn.Sign, level(k), -1.0)

    def beats(k):
        a, n = where(k)
        act(v("mv", a, a + n), v("ms", a, a + n), Fn.Relu, acc=v("lc", k, k + 1))

    def compare(k):
        a, n = where(k)
        ts(v("mv", a, a + n), v("cat", 16 * k + 192 - n, 16 * k + 192), level(k), Op.is_lt)

    def total(k):
        a, n = where(k)
        h = n // 2
        scan(v("sc", 96 * k + 96 - h, 96 * k + 96), v("mv", a, a + h), v("mv", a + h, a + n), 0.0, Op.add, Op.add)

    def piece(n):
        a, b, rows = PIECES[n]
        s = 224 if rows == [11] else 0
        quant(v("qm", a + s, b + s), v("sm", a + s, b + s), v("mv", 4 * a, 4 * b))
        for q in rows:
            o, c = 128 if q == 12 else 0, 96 * q + s
            mm(6, 128, v("qb", o, o + 128), v("sb", o, o + 128), v("qm", c, c + 128), v("sm", c, c + 128), q == 12, q == 11)

    end = {LO: C, 0: LO}

    def state(t, o, who, meanwhile=None):
        nxt, a = ("win%d" % t, 512 + 4 * o) if t < R else ("xlast", 4 * o)
        for q, b, lo, hi in who if t else []:
            f = 24 * b + o // 16
            out = v(nxt, a + 64 * lo + b, a + 64 * hi, 4)
            src = ind(v("win%d" % (t - 1), 0, 4 * (768 if t == 1 else 1536)), v("foff", f + lo, f + hi))
            if q == "S":
                act(out, src, Fn.Copy)
            else:
                cp(out, src)
        if meanwhile:
            meanwhile()
        quant(v("qx%d" % t, o, end[o]), v("sx%d" % t, o, end[o]), v(nxt, a, a + 4 * (end[o] - o)))

    for t in range(R):
        win = "win%d" % t
        msg, lmsg, lcnt = "msg%d" % t, "lmsg%d" % t, "lcnt%d" % t
        qx, sx = v("qx%d" % t), v("sx%d" % t)
        mean = 128 if t == 0 else 512
        wide = 768 if t == 0 else 1536

        def scores(bank, o):
            mm(bank, end[o] - o, v("qur"), v("sur"), v("qx%d" % t, o, end[o]), v("sx%d" % t, o, end[o]))

        def masked(bank, o):
            tt(v("pm", o, end[o]), v("ps%d" % bank, 0, end[o] - o), v("far", 0, end[o] - o), Op.add)

        def levels(o):
            scan(v("tb", o, end[o]), v("reset", 0, end[o] - o), v("pm", o, end[o]), 0.0, Op.add, Op.min)

        def within(bank, o):
            tt(v("mv", 12 * C + o, 12 * C + end[o]), v("ps%d" % bank, 0, end[o] - o), v("tb", o, end[o]), Op.is_gt)

        state(t, LO, UPPER)
        scores(4, LO)
        scores(5, LO)
        if t:
            send(peers[t], v("lqx%d" % t, LO, C), v("qx%d" % t, LO, C), "ax%d" % t, True)
        if t == 0:
            selectors()
        def upper():
            masked(4, LO)
            if t == 2:
                tt(v("inc"), v("sa", 2, 96, 4), pp, Op.min)
            levels(LO)

        state(t, 0, LOWER, upper)
        for bank in BANKS:
            scores(bank, 0)
        if t:
            send(peers[t], v("lqx%d" % t, 0, LO), v("qx%d" % t, 0, LO), "ax%d" % t, True)
            send(peers[t], v("lsx%d" % t), sx, "ax%d" % t)
        act(v("ab"), v("ps5", HI - 176, HI), Fn.Abs, 2.0 ** -124, 1.25 * 2.0 ** -24)
        act(v("cat", 192 + LO, 560), v("ps5", 0, 368 - LO), Fn.Copy)
        sign(23)
        sign(22)
        beats(23)
        act(v("cat", 192, 192 + LO), v("ps6", 0, LO), Fn.Copy)
        within(4, LO)
        tt(v("cat", 16, 192), v("ps4", HI - 176, HI), v("ab"), Op.subtract)
        if t == 0:
            quant(v("qb"), v("sb"), v("bt"))
        masked(7, 0)
        if t == 2:
            tt(pk, pk, v("inc"), Op.add)
        levels(0)
        ks, kv = KS, KV
        done = [23]

        def upto(a):
            while any(where(k)[0] < a for k in ks[len(done):]):
                j = len(done)
                if j + 1 < len(ks):
                    sign(ks[j + 1])
                beats(ks[j])
                done.append(ks[j])

        n = 0
        for j, k in enumerate(kv):
            compare(k)
            if j == 0:
                within(7, 0)
            else:
                total(kv[j - 1])
            if j == 1:
                scan(v("ds"), v("keep"), v("mv", 12 * C, 13 * C), 0.0, Op.mult, Op.add)
            while k == AFTER[n]:
                if n:
                    upto(4 * PIECES[n][1])
                piece(n)
                n += 1
        upto(NF)
        for h in range(2):
            act(v("cc", 12 * h, 12 * h + 12), v("ds", 192 * h + 15, 192 * h + 192, 16), Fn.Identity, v("cm", h, h + 1))
        total(kv[-1])
        piece(n)
        a, b = min(kv), max(kv) + 1
        tt(v("m96", 3 + 4 * a, 4 * b, 4), v("cc", a, b), v("sc", 95 + 96 * a, 96 * b, 96), Op.subtract)
        for a, b in ((0, a), (b, 24)):
            if a < b:
                tt(v("m96", 3 + 4 * a, 4 * b, 4), v("cc", a, b), v("lc", a, b), Op.subtract)
        if t == 0:
            ts(v("mc", 4, 5), v("mc", 3, 4), v("fp", 1, 2), Op.add, 2 * B, Op.add)
            spread("m4", 128, range(1))
        if t == 2:
            cp(v("cnt2", 24, 48), pk)
        scan(v("rs"), v("ps6", 0, 96), v("m96"), B, Op.min, Op.add)
        rk = v("rs", 3, 96, 4)
        place = v("cnt%d" % t, 0, 24)
        ts(place, rk, -B, Op.add)
        send(peers[t], v(lcnt), v("cnt%d" % t), "ac%d" % t)
        scatter(v("inv"), place, v("ids"))
        act(v("sw1"), rk, Fn.Sign, B + 127.5, -1.0)
        act(v("oa", 1, 48, 2), rk, Fn.Identity, B - 1000.0 * (B + 127), 1000.0)
        act(v("ob", 0, 48, 2), rk, Fn.Copy)
        act(v("wq"), v("sw1"), Fn.Relu, scale=field(rank))
        own = v("sb4", 3, 96, 4)
        if t == 0:
            for c in (1, 2, 3):
                act(v("m4", c, 128, 4), v("f192", 0, 32), Fn.Identity, v("mc", c + c // 3, c + c // 3 + 1), 0.0)
            act(v("ob", 1, 48, 2), v("f24"), Fn.Identity, v("fp", 0, 1))
            const(v("oa", 0, 48, 2), BB)

        def double_x(b):
            act(v(win, 4 * 640 + b, 4 * 1024, 4), v("ps%d" % b, 0, C), Fn.Copy, scale=2.0)

        if t:
            for b in range(3):
                mm(b, C, *half_tile(b), v("lqx%d" % t), v("lsx%d" % t))
                double_x(b)
        scan(v("sb4", 1, 96, 2), v("oa"), v("ob"), 0.0, Op.max, Op.min)
        scan(v("s4"), v("inv", 0, 128), v("m4"), B, Op.min, Op.add)
        if t:
            ts(v(msg, 32, 56), own, -B, Op.add)
        ts(v(msg, 0, 32), v("s4", 3, 128, 4), -B, Op.add)
        send(peers[t], v(lmsg), v(msg), "am%d" % t)

        xs = v(win, 512, 2048)
        act(v("zt", ZS[t], 512), ind(xs, v(msg, ZS[t] // 16, 32)), Fn.Copy)
        if t:
            mm(3, C, *half_tile(3), v("lqx%d" % t), v("lsx%d" % t))
            double_x(3)
        cp(v("zt", 0, ZS[t]), ind(xs, v(msg, 0, ZS[t] // 16)))
        early = []
        if t:
            early += [lambda: ts(v("gm", 0, 24), v(lcnt, 0, 24), 128.0, Op.is_lt, field(rank ^ STEP[t]), Op.mult),
                      lambda: ts(v("gm", 24, 48), v(lcnt, 24, 48), -float(GUARD) * (t - 1), Op.add),
                      lambda: tt(pk, pk, v("wq"), Op.add),
                      lambda: tt(pp, v("gm", 0, 24), v("gm", 24, 48), Op.add),
                      lambda: offsets("xoff", own, 1)]
        if t == 1:
            early += [lambda: ts(v("nwu"), pp, 0.0, Op.is_equal)]
        if t == 2:
            early += [lambda: tt(v("dd", 24, 48), pk, pp, Op.subtract),
                      lambda: offsets("xoff", own, 3),
                      lambda: ts(v("an", 24, 48), v("dd", 24, 48), GUARD, Op.bitwise_and),
                      lambda: offsets("xoff", own, 0),
                      lambda: ts(v("nwu"), v("an", 24, 48), float(GUARD), Op.is_equal)]
        if t == 0:
            early += [lambda b=b: offsets("xoff", own, b) for b in (1, 3, 0, 2)] + [lambda: tt(pk, pk, v("wq"), Op.add)]
            early += [lambda: [fill(v(name, a, 96, 4), c) for name, a, c in (("sa", 0, -BB), ("sb4", 2, -BB), ("sa", 2, BB))]]
        for call in early[:E1[t]]:
            call()
        quant(v("qz"), v("sz"), v("zt"))
        for b in range(4):
            mm(4 + b, A, v("qw", 128 * b, 128 * b + 128), v("sw", 128 * b, 128 * b + 128), v("qz"), v("sz"))
        for b in range(4):
            act(v("rr", b, 512, 4), v("ps%d" % (4 + b), 0, A), Fn.Relu, scale=0.03125)
        for call in early[E1[t]:E2[t]]:
            call()
        late = early[E2[t]:]

        def wanted():
            act(v("wr"), ind(v("tab"), v("nwu")), Fn.Copy)

        both, far_mean, far_d, cut_at, want = v("sb4", 0, 96, 4), v("sa", 1, 96, 4), v("sb4", 1, 96, 4), v("sa", 2, 96, 4), v("sa", 3, 96, 4)
        if t == 0:
            act(both, v("sw1"), Fn.Relu, scale=BB)
            act(v("c2"), v("ob", 1, 48, 2), Fn.Identity, -2 * B - 256.0 - (C + K), 2.0)
            for j in range(3):
                const(v("w4", j + 1, 192, 4), 4.0 ** (high[j] - high[j + 1]))
        if t:
            wanted()
        for b in range(4):
            tt(v(win, b, 512, 4), v("rr", b, 512, 4), v("zt", b, 512, 4), Op.add)
        quant(v("qh%d" % t), v("sh%d" % t), v(win, 0, 512))
        send(peers[t], v("lqh%d" % t), v("qh%d" % t), "ah%d" % t, True)
        send(peers[t], v("lsh%d" % t), v("sh%d" % t), "ah%d" % t)

        def halve(b, q):
            src = ind(v(win, 0, 2048), v("xoff", 24 * b, 24 * b + 24))
            if q == "V":
                ts(v("xh", b, 4 * C, 4), src, 0.5, Op.mult)
            else:
                act(v("xh", b, 4 * C, 4), src, Fn.Copy, scale=0.5)

        def mean_x(b):
            tt(v(win, 4 * 1152 + b, 4 * 1536, 4), v("ps%d" % b, 0, C), v("xh", b, 4 * C, 4), Op.add)

        def cut():
            scan(v("pre"), v("wr"), v("wr"), 0.0, Op.add, Op.max)
            act(v("sg", K, C), v("pre", K, C), Fn.Sign, K + 0.5, -1.0, v("acc"))

        halve(1, "S")
        if t == 0:
            for call in late:
                call()
            halve(0, "V")
            halve(3, "S")
            halve(2, "V")
            act(v("oh"), ind(v("xh"), v(lmsg, 0, 32)), Fn.Copy)
            ts(far_d, v(lcnt), 512.0 + B, Op.add)
            ts(far_mean, v(lcnt), 512.0 + B + mean, Op.add)
            ts(want, v(lcnt), 128.0, Op.is_lt, BB, Op.mult)
            for b in range(4):
                o = 516 * (b % 2) + 2 - b // 2 * 2
                quant(*half_tile(b), v("et", o, o + 512))
                if b == 0:
                    scan(v("so"), v("sa"), v("sb4"), 0.0, Op.min, Op.max)
            quant(v("qv"), v("sv"), v("vt"))
            ts(v("inc"), v(lcnt), 128.0, Op.is_lt, field(rank ^ STEP[0]), Op.mult)
        else:
            for b in (0, 3)[:2 * (2 - t)]:
                offsets("xoff", own, b)
            cut()
            offsets("xoff", own, 2)
            if t == 2:
                ts(v("dd", 0, 24), v("dd", 24, 48), -1.0, Op.mult, 2.0 * GUARD, Op.add)
            halve(0, "V")
            halve(3, "S")
            halve(2, "S")
            act(v("oh", OV, 512), ind(v("xh"), v(lmsg, OV // 16, 32)), Fn.Copy)
            if t == 1:
                ts(both, pk, BB, Op.mult)
                ts(want, pp, BB, Op.mult)
            if t == 2:
                ts(v("an", 0, 24), v("dd", 0, 24), GUARD, Op.bitwise_and)
                ts(want, v("an", 24, 48), float(GUARD), Op.not_equal, BB, Op.mult)
            ts(far_d, v(lmsg, 32, 56), 512.0 + B, Op.add)
            mean_x(1)
            ts(far_mean, v(lmsg, 32, 56), 512.0 + B + mean, Op.add)
            ts(cut_at, v("c2"), v("acc"), Op.is_lt, BB, Op.mult)
            if t == 2:
                ts(both, v("an", 0, 24), float(GUARD), Op.not_equal, BB, Op.mult)
            mean_x(0)
            scan(v("so"), v("sa"), v("sb4"), 0.0, Op.min, Op.max)
            mean_x(3)
            if t == 2:
                tt(v("recv"), cut_at, want, Op.min)
        for b in range(4):
            offsets("foff", v("so", 3, 96, 4), b)
        if t:
            mean_x(2)
            cp(v("oh", 0, OV), ind(v("xh"), v(lmsg, 0, OV // 16)))
        if t == 0:
            tt(pk, pk, v("inc"), Op.add)
            constants()
            cp(v("cnt1", 24, 48), pk)


        for b in range(4):
            mm(4 + b, A, *half_tile(b), v("lqh%d" % t), v("lsh%d" % t))
        for b in range(4):
            o = 4 * (512 + mean)
            whole, halves = v(win, 4 * 512 + b, 4 * 640, 4), v("ps%d" % (4 + b), 0, A)
            if DH[b] == "S":
                act(whole, halves, Fn.Copy, scale=2.0)
            tt(v(win, o + b, o + 512, 4), halves, v("oh", b, 512, 4), Op.add)
            if DH[b] == "s":
                act(whole, halves, Fn.Copy, scale=2.0)
            if DH[b] == "v":
                ts(whole, halves, 2.0, Op.mult)

    qx, sx = v("qx%d" % R), v("sx%d" % R)

    def fields():
        for j in range(4):
            ts(v("un", j, 192, 4), v("de"), 4 * coset.index(high[j] ^ first), Op.logical_shift_right, 7, Op.bitwise_and)
        ts(v("uf"), v("un"), -4.0, Op.add, 0.0, Op.max)

    def pairs():
        tt(v("de", 1, 48, 2), v("dd", 0, 24), v("recv"), Op.min)
        ts(v("de", 0, 48, 2), pk, float(GUARD), Op.add)

    for bank, o, who, meanwhile in ((4, LO, UPPER, pairs), (5, 0, LAST, fields)):
        state(R, o, who, meanwhile)
        mm(bank, end[o] - o, v("qv"), v("sv"), v("qx%d" % R, o, end[o]), v("sx%d" % R, o, end[o]))
    act(v("ysb", LO, C), v("ps4", 0, HI), Fn.Copy)
    dma("Y", T.oc[:], qx[0].bitcast(dt.uint8), "outy", reads=qx[1])
    act(v("ysb", 0, LO), v("ps5", 0, LO), Fn.Copy)
    dma("S", T.y[:], v("ysb")[0], "outs", reads=v("ysb")[1])
    for k in range(4):
        q, sem = ("S", "outs") if k == 3 else ("Y", "outy")
        dma(q, T.osc[4 * k:4 * k + 4, :], T["sx%d" % R][32 * k:32 * k + 4, :], sem, reads=sx[1])
    scan(v("ug"), v("w4"), v("uf"), 0.0, Op.mult, Op.add)
    ts(v("ovb", 0, 24), v("ug", 7, 192, 8), float(4 ** high[3]), Op.mult)
    run("V", lambda: g.vector.transpose(v("ovt")[0], v("ovb")[0]), v("ovt"), [v("ovb")])
    for k in range(8):
        q, sem = ("S", "outs") if k % 2 else ("Y", "outy")
        a, h = k // 2, k % 2
        dma(q, T.ov[k:k + 1, :], T["ovt"][32 * a:32 * a + 24, 16 * h:16 * h + 16], sem, reads=v("ovt")[1])
    wait("G", "G", count["G"])
    wait("G", "sent", count["sent"])
    wait("P", "P", count["P"])
    wait("Y", "outy", count["outy"])
    wait("S", "outs", count["outs"])
